import numpy as np
import ml_dtypes


def mxq(x, axis, fmt="e4m3"):
    dtype, down = {"e4m3": (ml_dtypes.float8_e4m3fn, 7), "e5m2": (ml_dtypes.float8_e5m2, 14)}[fmt]
    v = np.moveaxis(np.asarray(x, np.float32).astype(ml_dtypes.bfloat16).astype(np.float64), axis, -1)
    blocks = v.reshape(v.shape[:-1] + (-1, 32))
    amax = np.abs(blocks).max(-1, keepdims=True)
    byte = np.maximum(np.where(amax > 0, np.frexp(amax)[1] - 1 + 127, 0) - down, 1)
    scale = np.exp2(byte - 127.0)
    codes = (blocks / scale).astype(np.float32).astype(dtype).astype(np.float64)
    return np.moveaxis((codes * scale).reshape(v.shape), -1, axis)


WIDE = False


def mx_kscale(k):
    if not WIDE:
        return np.ones(k)
    levels = np.array([18, -18])
    if k % 512:
        return np.exp2(np.random.permutation(np.resize(levels, k // 32))).repeat(32)
    a = np.empty((k // 512, 16))
    for p in range(k // 512):
        a[p, :8] = np.random.permutation(np.resize(levels, 8))
        for g in range(8):
            far = levels[np.abs(levels - a[p, g]) >= 10]
            a[p, g + 8] = far[np.random.randint(len(far))]
    return np.exp2(a.ravel()).repeat(32)


def f64(x):
    return np.asarray(x).astype(np.float64)


def striped(idx):
    return np.tile(np.asarray(idx).reshape(-1, 16).T, (8, 1)).astype(np.uint16)


def unstriped(offs):
    return offs[:16].T.reshape(-1).astype(np.int64)


E2M1 = np.array([0.0, 0.5, 1.0, 1.5, 2.0, 3.0, 4.0, 6.0, -0.0, -0.5, -1.0, -1.5, -2.0, -3.0, -4.0, -6.0])


def pack_weight(w, fmt):
    k, n = w.shape
    w = f64(np.asarray(w, np.float32).astype(ml_dtypes.bfloat16)).reshape(k // 32, 32, n)
    amax = np.abs(w).max(1)
    if fmt == "e4m3":
        byte = np.frexp(amax)[1] - 1 + 127 - 7
    else:
        mant, ex = np.frexp(amax / 6.0)
        byte = np.where(mant > 0.5, ex, ex - 1) + 127
    byte = np.clip(np.where(amax > 0, byte, 1), 1, 254)
    scaled = (w * np.exp2(127.0 - byte)[:, None, :]).reshape(k, n).astype(np.float32)
    by_word = np.ascontiguousarray(scaled.reshape(k // 512, 128, 4, n).transpose(0, 1, 3, 2))
    if fmt == "e4m3":
        words = by_word.astype(ml_dtypes.float8_e4m3fn).view(np.uint8)
    else:
        c = by_word.astype(ml_dtypes.float4_e2m1fn).view(np.uint8) & 0xF
        words = (c[..., 0::2] | (c[..., 1::2] << 4)).reshape(k // 512, 128, 2 * n)
    return np.ascontiguousarray(words), np.ascontiguousarray(byte.astype(np.uint8).reshape(k // 512, 16, n))


def unpack_weight(words, scales, fmt):
    g, _, n = scales.shape
    words = np.ascontiguousarray(words).reshape(g, 128, n, -1)
    if fmt == "e4m3":
        vals = words.view(ml_dtypes.float8_e4m3fn).astype(np.float64)
    else:
        nib = np.empty((g, 128, n, 4), np.uint8)
        nib[..., 0::2] = words & 0xF
        nib[..., 1::2] = words >> 4
        vals = E2M1[nib]
    vals = vals * np.repeat(np.exp2(scales.astype(np.float64) - 127.0), 8, axis=1)[..., None]
    return vals.transpose(0, 1, 3, 2).reshape(g * 512, n)


B, N, T, D, DV, R = 1, 512, 2048, 512, 512, 1024


def setup_inputs():
    n = np.random.standard_normal
    idx = np.random.permutation(T)[:B * N]
    s = mx_kscale(D)[:, None]
    z = mx_kscale(R)[:, None]
    v = mx_kscale(DV)[:, None]
    q = n((B, D, R))
    do = n((B, DV, R))
    kp = pack_weight(n((D, T)) * (0.50 / np.sqrt(D)) / s, "e4m3")
    vp = pack_weight(n((DV, T)) / np.sqrt(DV) / v, "e4m3")
    return {
        "qT": (q * s).astype(np.float32),
        "k_words": kp[0],
        "k_scales": kp[1],
        "v_words": vp[0],
        "v_scales": vp[1],
        "doT": (do * v).astype(np.float32),
        "lse": (np.log(N) + 0.12 + 0.1 * n((B, R, 1))).astype(np.float32),
        "delta": (0.3 * n((B, R, 1))).astype(np.float32),
        "rw": (np.random.uniform(0.5, 1.5, (B, R, 1)) * N / np.sqrt(R) * z).astype(np.float32),
        "qm": (q.transpose(0, 2, 1) / z).astype(np.float32),
        "offs": striped(idx),
    }


def reference(qT, k_words, k_scales, v_words, v_scales, doT, lse, delta, rw, qm, offs):
    idx = unstriped(offs)
    v = unpack_weight(v_words, v_scales, "e4m3")
    k = unpack_weight(k_words, k_scales, "e4m3")
    pick = lambda x: x[:, idx].reshape(x.shape[0], B, N).transpose(1, 0, 2)
    a = mxq(f64(qT), 1, "e4m3").transpose(0, 2, 1) @ pick(k)
    p = np.exp(a - f64(lse))
    dp = mxq(f64(doT), 1, "e5m2").transpose(0, 2, 1) @ pick(v)
    ds = f64(rw) * p * (dp - f64(delta))
    dk = mxq(f64(qm), 1, "e4m3").transpose(0, 2, 1) @ mxq(ds, 1, "e5m2")
    gk = np.zeros((D, T))
    gk[:, idx] = dk.transpose(1, 0, 2).reshape(D, B * N)
    return gk

@@ -1,0 +1,257 @@
+from contextlib import ExitStack
+
+import concourse.mybir as mybir
+
+N, T, D, R = 512, 2048, 512, 1024
+FLOPS = 3 * 2 * R * N * D
+
+F32 = mybir.dt.float32
+BF16 = mybir.dt.bfloat16
+I32 = mybir.dt.int32
+U32 = mybir.dt.uint32
+U16 = mybir.dt.uint16
+U8 = mybir.dt.uint8
+E4 = mybir.dt.float8_e4m3fn_x4
+E5 = mybir.dt.float8_e5m2_x4
+ALU = mybir.AluOpType
+ACT = mybir.ActivationFunctionType
+
+P = 128
+PACK = 4
+KP = P * PACK
+G = R // KP
+
+
+def tile_attend_gat_lse_k_kernel(
+    tc, qT, k_words, k_scales, v_words, v_scales, doT, lse, delta, rw, qm, offs, out
+):
+    nc = tc.nc
+    with ExitStack() as ctx:
+        keep = ctx.enter_context(tc.tile_pool(name="keep", bufs=1))
+        psum = ctx.enter_context(tc.psum_pool(name="psum", bufs=1))
+
+        def sb(name, shape, dtype):
+            return keep.tile(shape, dtype, name=name, align_bytes=64)
+
+        CFG = {"nw":3,"wG":True,"vf":True,"loads":["vw","vs0","vs1","vs2","vs3","offs","delta","d0","rw","ks0","ks1","ks2","ks3","q0","lse","kw","d1","q1a","q1b","qm00","qm10","qm01","qm11"],"order":["cd1","cq0","gkw","cd0","gks","gvs","Qd0","cq1","gvw","nd","W0","Qd1","nl","Qq0","E0","W1","cm01","Qq1","cm00","E1","cm11","cm10","M1","M0","cm21","cm20","Qm2","Qs0","Qm0","Qs1","Qm1","K0","X0","K1","cm31","cm30","X1","K2","Qm3","X2","K3","X3"],"eng":{"w00":"S","cm00":"V","w01":"S","cm10":"S","w02":"S","cm20":"S","w03":"S","cm30":"S","w10":"S","cm01":"V","w11":"S","cm11":"S","w12":"S","cm21":"S","w13":"S","cm31":"S","ek0":"S","ek1":"S","ek2":"S","ek3":"S"},"calls":{"Qq0":1,"Qq1":1,"Qd0":1,"Qd1":4},"ns":{"q0":1,"q1":0,"d0":2,"d1":0},"sp":{"E0":1,"W0":1,"E1":2,"W1":1},"mc":{"0":1,"1":2},"il":{"0":1,"1":1}}
+        offsets = keep.tile([P, N // 16], U16, name="offsets")
+        pool_scales = {}
+        for name in (("v", "k") if CFG["vf"] else ("k", "v")):
+            pool_scales[name] = sb(name + "_pool_scales", [P, T // 4], I32)
+            nc.gpsimd.memset(pool_scales[name][:], 0)
+        warm = sb("warm", [P, 2], F32)
+        nc.gpsimd.memset(warm[:, 0:1], 0.0)
+        nc.scalar.activation(warm[:, 1:2], warm[:, 0:1], ACT.Exp)
+        windows = []
+        for w in range(CFG["nw"]):
+            windows.append(sb("window%d" % w, [P, T], F32))
+            if CFG["wG"] and w == CFG["nw"] - 1:
+                nc.gpsimd.memset(windows[w][:], 0.0)
+            else:
+                nc.vector.memset(windows[w][:], 0.0)
+
+        def load_rows(name, src, c0, width):
+            tile = sb(name, [P, PACK, width], F32)
+            nc.sync.dma_start(tile[:], src.rearrange("(p j) c -> p j c", j=PACK)[:, :, c0 : c0 + width])
+            return tile
+
+        cols = {}
+        pool_words = {}
+        raw = {}
+        qm_raw = {}
+        for x in CFG["loads"]:
+            if x == "offs":
+                nc.sync.dma_start(offsets[:], offs)
+            elif x in ("lse", "delta", "rw"):
+                src = {"lse": lse, "delta": delta, "rw": rw}[x]
+                cols[x] = sb(x + "_cols", [P, G, PACK], F32)
+                nc.sync.dma_start(cols[x][:], src[0].rearrange("(g p t) o -> p g (t o)", g=G, t=PACK))
+            elif x in ("kw", "vw"):
+                pool_words[x[0]] = sb(x + "_pool_words", [P, T], I32)
+                src = k_words if x == "kw" else v_words
+                nc.sync.dma_start(pool_words[x[0]][:], src[0].rearrange("p t j -> p (t j)").bitcast(I32))
+            elif x[:2] in ("ks", "vs"):
+                r = int(x[2])
+                src = k_scales if x[0] == "k" else v_scales
+                nc.sync.dma_start(pool_scales[x[0]][r:P:32, :], src[0, r:16:4, :].bitcast(I32))
+            elif x[:2] == "qm":
+                g, h = int(x[2]), int(x[3])
+                qm_raw[g, h] = load_rows(x, qm[0, g * KP : (g + 1) * KP, :], h * 256, 256)
+            else:
+                width = {1: 1024, 2: 512, 3: 256}[len(x)]
+                c0 = 0
+                if len(x) > 1:
+                    c0 += int(x[1]) * KP
+                if len(x) > 2:
+                    c0 += 256 * (x[2] == "b")
+                tile = load_rows("raw_" + x, qT[0] if x[0] == "q" else doT[0], c0, width)
+                for quarter in range(width // P):
+                    raw[x[0], c0 // P + quarter] = (x, tile, quarter * P)
+
+        def flat(tile):
+            return tile[:].rearrange("p a b c -> p (a b c)")
+
+        def bank(b):
+            return psum.tile([P, N], F32, name="bank%d" % b, tag="bank%d" % b)
+
+        def copy_on(engine, dst, src):
+            if engine == "S":
+                nc.scalar.copy(dst, src)
+            else:
+                nc.vector.tensor_copy(dst, src)
+
+        def quantize(name, grouped, fmt, calls):
+            codes = sb(name + "_codes", [P, KP], U32)
+            scales = sb(name + "_scales", [P, KP], U8)
+            w = KP // calls
+            for c in range(calls):
+                nc.vector.quantize_mx(
+                    out=codes[:, c * w : (c + 1) * w].bitcast(fmt),
+                    scales=scales[:, c * w : (c + 1) * w],
+                    in_=grouped[:, PACK * c * w : PACK * (c + 1) * w],
+                )
+            return codes, scales
+
+        def product(b, stat, t, fmt, pool):
+            acc = bank(b)
+            nc.tensor.matmul_mx(
+                out=acc[:],
+                lhsT=stat[0][:, t * P : (t + 1) * P].bitcast(fmt),
+                lhsT_scale=stat[1][:, t * P : (t + 1) * P],
+                rhs=made["g" + pool + "w"][:].bitcast(E4),
+                rhs_scale=made["g" + pool + "s"][:],
+                start=True,
+                stop=True,
+            )
+            return acc
+
+        made = {}
+        p_t = [sb("p%d" % g, [P, PACK, N], F32) for g in range(G)]
+        w_t = [sb("w%d" % g, [P, PACK, N], F32) for g in range(G)]
+        gm = [sb("gm%d" % m, [P, G, P, PACK], BF16) for m in range(4)]
+        stores = 0
+        for s in CFG["order"]:
+            if s == "nl":
+                made[s] = sb("neg_lse", [P, G, PACK], F32)
+                nc.vector.tensor_scalar(made[s][:], cols["lse"][:], -1.0, None, ALU.mult)
+            elif s == "nd":
+                made[s] = sb("neg_delta_rw", [P, G, PACK], F32)
+                nc.vector.scalar_tensor_tensor(made[s][:], cols["delta"][:], -1.0, cols["rw"][:], ALU.mult, ALU.mult)
+            elif s in ("gks", "gvs"):
+                made[s] = sb(s, [P, N], U8)
+                nc.vector.tensor_copy(made[s][:], pool_scales[s[1]][:].bitcast(U8).indirect(offsets[:]))
+            elif s in ("gkw", "gvw"):
+                made[s] = sb(s, [P, N], U32)
+                nc.vector.tensor_copy(made[s][:], pool_words[s[1]][:].bitcast(U32).indirect(offsets[:]))
+            elif s[0] == "c" and s[1] in "qd":
+                g = int(s[2])
+                grouped = sb(s, [P, PACK, P, PACK], BF16)
+                made[s] = grouped
+                pieces = []
+                for i in range(4):
+                    e = "S" if i < CFG["ns"][s[1:]] else "V"
+                    x, tile, c0 = raw[s[1], 4 * g + i]
+                    if pieces and pieces[-1][0] == e and pieces[-1][1] == x:
+                        pieces[-1][4] += P
+                    else:
+                        pieces.append([e, x, tile, c0, P, i])
+                for e, x, tile, c0, width, i in pieces:
+                    copy_on(
+                        e,
+                        grouped[:, :, 32 * i : 32 * i + width // PACK, :].rearrange("p t m j -> p m j t"),
+                        tile[:, :, c0 : c0 + width].rearrange("p j (m t) -> p m j t", t=PACK),
+                    )
+            elif s[0] == "Q" and s[1] in "qd":
+                made[s] = quantize(s, flat(made["c" + s[1:]]), E4 if s[1] == "q" else E5, CFG["calls"][s])
+            elif s[0] in "EW":
+                g = int(s[1])
+                sp = CFG["sp"][s]
+                accs = []
+                for h in range(sp):
+                    c = slice(h * N // sp, (h + 1) * N // sp)
+                    for t in range(PACK):
+                        if h == 0:
+                            if s[0] == "E":
+                                accs.append(product(t, made["Qq%d" % g], t, E4, "k"))
+                            else:
+                                accs.append(product(PACK + t, made["Qd%d" % g], t, E5, "v"))
+                        acc = accs[t]
+                        if s[0] == "E":
+                            nc.scalar.activation(p_t[g][:, t, c], acc[:, c], ACT.Exp, bias=made["nl"][:, g, t : t + 1])
+                        elif CFG["eng"]["w%d%d" % (g, t)] == "V":
+                            nc.vector.tensor_scalar(
+                                w_t[g][:, t, c], acc[:, c], cols["delta"][:, g, t : t + 1], cols["rw"][:, g, t : t + 1],
+                                ALU.subtract, ALU.mult,
+                            )
+                        else:
+                            nc.scalar.activation(
+                                w_t[g][:, t, c], acc[:, c], ACT.Identity,
+                                bias=made["nd"][:, g, t : t + 1], scale=cols["rw"][:, g, t : t + 1],
+                            )
+            elif s[0] == "M" or s[:2] == "Qs":
+                g = int(s[-1])
+                mc = CFG["mc"][s[-1]]
+                wide = N // mc
+                if s[0] == "M":
+                    made[s] = sb("ds%d" % g, [P, N, PACK], BF16)
+                    made["Qs%d" % g] = (sb("ds_codes%d" % g, [P, N], U32), sb("ds_scales%d" % g, [P, N], U8))
+                ds = made["M%d" % g]
+                todo = []
+                if s[0] == "M":
+                    for h in range(mc):
+                        todo.append(("m", h))
+                        if CFG["il"][s[-1]] and h > 0:
+                            todo.append(("q", h - 1))
+                else:
+                    for h in range(mc - 1 if CFG["il"][s[-1]] else 0, mc):
+                        todo.append(("q", h))
+                for kind, h in todo:
+                    c = slice(h * wide, (h + 1) * wide)
+                    if kind == "m":
+                        nc.vector.tensor_tensor(
+                            ds[:, c, :].rearrange("p (c i) t -> p c t i", i=4),
+                            p_t[g][:, :, c].rearrange("p t (c i) -> p c t i", i=4),
+                            w_t[g][:, :, c].rearrange("p t (c i) -> p c t i", i=4),
+                            ALU.mult,
+                        )
+                    else:
+                        nc.vector.quantize_mx(
+                            out=made["Qs%d" % g][0][:, c].bitcast(E5),
+                            scales=made["Qs%d" % g][1][:, c],
+                            in_=ds[:, c, :].rearrange("p i t -> p (i t)"),
+                        )
+            elif s[:2] == "cm":
+                m, g = int(s[2]), int(s[3])
+                h, c0 = divmod(m * P, 256)
+                copy_on(
+                    CFG["eng"][s],
+                    gm[m][:, g, :, :].rearrange("p (c i) t -> p c t i", i=4),
+                    qm_raw[g, h][:, :, c0 : c0 + P].rearrange("p t (c i) -> p c t i", i=4),
+                )
+            elif s[:2] == "Qm":
+                codes = sb(s + "_codes", [P, G * P], U32)
+                scales = sb(s + "_scales", [P, G * P], U8)
+                nc.vector.quantize_mx(out=codes[:].bitcast(E4), scales=scales[:], in_=flat(gm[int(s[2])]))
+                made[s] = (codes, scales)
+            elif s[0] == "K":
+                m = int(s[1])
+                codes, scales = made["Qm%d" % m]
+                acc = bank(m)
+                for g in range(G):
+                    nc.tensor.matmul_mx(
+                        out=acc[:],
+                        lhsT=codes[:, g * P : (g + 1) * P].bitcast(E4),
+                        lhsT_scale=scales[:, g * P : (g + 1) * P],
+                        rhs=made["Qs%d" % g][0][:].bitcast(E5),
+                        rhs_scale=made["Qs%d" % g][1][:],
+                        start=(g == 0),
+                        stop=(g == G - 1),
+                    )
+                made[s] = sb("dk%d" % m, [P, N], F32)
+                copy_on(CFG["eng"]["ek%d" % m], made[s][:], acc[:])
+            elif s[0] == "X":
+                m = int(s[1])
+                window = windows[stores % len(windows)]
+                stores += 1
+                nc.vector.tensor_copy(window[:].indirect(offsets[:]), made["K%d" % m][:])
+                nc.sync.dma_start(out[m * P : (m + 1) * P, :], window[:])

@@ -33,7 +33,7 @@ def tile_attend_gat_lse_k_kernel(
         def sb(name, shape, dtype):
             return keep.tile(shape, dtype, name=name, align_bytes=64)
 
-        CFG = {"nw":3,"wG":True,"vf":True,"loads":["vw","vs0","vs1","vs2","vs3","offs","delta","d0","rw","ks0","ks1","ks2","ks3","q0","lse","kw","d1","q1a","q1b","qm00","qm10","qm01","qm11"],"order":["cd1","cq0","gkw","cd0","gks","gvs","Qd0","cq1","gvw","nd","W0","Qd1","nl","Qq0","E0","W1","cm01","Qq1","cm00","E1","cm11","cm10","M1","M0","cm21","cm20","Qm2","Qs0","Qm0","Qs1","Qm1","K0","X0","K1","cm31","cm30","X1","K2","Qm3","X2","K3","X3"],"eng":{"w00":"S","cm00":"V","w01":"S","cm10":"S","w02":"S","cm20":"S","w03":"S","cm30":"S","w10":"S","cm01":"V","w11":"S","cm11":"S","w12":"S","cm21":"S","w13":"S","cm31":"S","ek0":"S","ek1":"S","ek2":"S","ek3":"S"},"calls":{"Qq0":1,"Qq1":1,"Qd0":1,"Qd1":4},"ns":{"q0":1,"q1":0,"d0":2,"d1":0},"sp":{"E0":1,"W0":1,"E1":2,"W1":1},"mc":{"0":1,"1":2},"il":{"0":1,"1":1}}
+        CFG = {"nw":3,"wG":True,"vf":True,"loads":["offs","vs0","vs1","vs2","vs3","delta","rw","d0","ks0","ks1","ks2","ks3","vw","lse","q0","kw","d1","q1a","q1b","qm00","qm10","qm01","qm11"],"order":["gvs","gks","cd0","Qd0","nd","gvw","W0","nl","cq0","gkw","Qq0","E0","cd1","Qd1","W1","cq1","Qq1","E1","M0","cm00","cm01","Qs0","Qm0","M1","Qs1","K0","cm10","cm11","Qm1","K1","cm20","cm21","Qm2","K2","cm30","cm31","Qm3","K3","X0","X1","X2","X3"],"eng":{"w00":"S","cm00":"V","w01":"S","cm10":"S","w02":"S","cm20":"S","w03":"S","cm30":"S","w10":"S","cm01":"V","w11":"S","cm11":"S","w12":"S","cm21":"S","w13":"S","cm31":"S","ek0":"S","ek1":"S","ek2":"S","ek3":"S"},"calls":{"Qq0":2,"Qq1":2,"Qd0":2,"Qd1":2},"ns":{"q0":0,"q1":0,"d0":3,"d1":0},"sp":{"E0":1,"W0":1,"E1":2,"W1":1},"mc":{"0":2,"1":2},"il":{"0":0,"1":0},"gate":{"d1":None,"q1a":"q0","q1b":"q0","qm00":"d1","qm10":"d1","qm01":"q1","qm11":"q1"}}
         offsets = keep.tile([P, N // 16], U16, name="offsets")
         pool_scales = {}
         for name in (("v", "k") if CFG["vf"] else ("k", "v")):
@@ -50,22 +50,31 @@ def tile_attend_gat_lse_k_kernel(
             else:
                 nc.vector.memset(windows[w][:], 0.0)
 
+        used = {}
+
         def load_rows(name, src, c0, width):
-            tile = sb(name, [P, PACK, width], F32)
-            nc.sync.dma_start(tile[:], src.rearrange("(p j) c -> p j c", j=PACK)[:, :, c0 : c0 + width])
-            return tile
+            y = CFG["gate"].get(name.replace("raw_", ""))
+            if y:
+                tile = raw[y[0], 4 * int(y[1])][1]
+                at = used.get(y, 0)
+                used[y] = at + width
+            else:
+                tile = sb(name, [P, PACK, width], F32)
+                at = 0
+            nc.sync.dma_start(tile[:, :, at : at + width], src.rearrange("(p j) c -> p j c", j=PACK)[:, :, c0 : c0 + width])
+            return tile, at
 
         cols = {}
         pool_words = {}
         raw = {}
         qm_raw = {}
-        for x in CFG["loads"]:
+        def load(x):
             if x == "offs":
                 nc.sync.dma_start(offsets[:], offs)
             elif x in ("lse", "delta", "rw"):
                 src = {"lse": lse, "delta": delta, "rw": rw}[x]
-                cols[x] = sb(x + "_cols", [P, G, PACK], F32)
-                nc.sync.dma_start(cols[x][:], src[0].rearrange("(g p t) o -> p g (t o)", g=G, t=PACK))
+                cols[x] = sb(x + "_cols", [P, G, 2 * PACK], F32)[:, :, 0:PACK]
+                (nc.gpsimd if CFG.get("vecG") else nc.sync).dma_start(cols[x], src[0].rearrange("(g p t) o -> p g (t o)", g=G, t=PACK))
             elif x in ("kw", "vw"):
                 pool_words[x[0]] = sb(x + "_pool_words", [P, T], I32)
                 src = k_words if x == "kw" else v_words
@@ -84,9 +93,13 @@ def tile_attend_gat_lse_k_kernel(
                     c0 += int(x[1]) * KP
                 if len(x) > 2:
                     c0 += 256 * (x[2] == "b")
-                tile = load_rows("raw_" + x, qT[0] if x[0] == "q" else doT[0], c0, width)
+                tile, at = load_rows("raw_" + x, qT[0] if x[0] == "q" else doT[0], c0, width)
                 for quarter in range(width // P):
-                    raw[x[0], c0 // P + quarter] = (x, tile, quarter * P)
+                    raw[x[0], c0 // P + quarter] = (x, tile, at + quarter * P)
+
+        for x in CFG["loads"]:
+            if not CFG["gate"].get(x):
+                load(x)
 
         def flat(tile):
             return tile[:].rearrange("p a b c -> p (a b c)")
@@ -133,10 +146,10 @@ def tile_attend_gat_lse_k_kernel(
         for s in CFG["order"]:
             if s == "nl":
                 made[s] = sb("neg_lse", [P, G, PACK], F32)
-                nc.vector.tensor_scalar(made[s][:], cols["lse"][:], -1.0, None, ALU.mult)
+                nc.vector.tensor_scalar(made[s][:], cols["lse"], -1.0, None, ALU.mult)
             elif s == "nd":
                 made[s] = sb("neg_delta_rw", [P, G, PACK], F32)
-                nc.vector.scalar_tensor_tensor(made[s][:], cols["delta"][:], -1.0, cols["rw"][:], ALU.mult, ALU.mult)
+                nc.vector.scalar_tensor_tensor(made[s][:], cols["delta"], -1.0, cols["rw"], ALU.mult, ALU.mult)
             elif s in ("gks", "gvs"):
                 made[s] = sb(s, [P, N], U8)
                 nc.vector.tensor_copy(made[s][:], pool_scales[s[1]][:].bitcast(U8).indirect(offsets[:]))
@@ -161,6 +174,9 @@ def tile_attend_gat_lse_k_kernel(
                         grouped[:, :, 32 * i : 32 * i + width // PACK, :].rearrange("p t m j -> p m j t"),
                         tile[:, :, c0 : c0 + width].rearrange("p j (m t) -> p m j t", t=PACK),
                     )
+                for x in CFG["loads"]:
+                    if CFG["gate"].get(x) == s[1:]:
+                        load(x)
             elif s[0] == "Q" and s[1] in "qd":
                 made[s] = quantize(s, flat(made["c" + s[1:]]), E4 if s[1] == "q" else E5, CFG["calls"][s])
             elif s[0] in "EW":
@@ -223,10 +239,11 @@ def tile_attend_gat_lse_k_kernel(
             elif s[:2] == "cm":
                 m, g = int(s[2]), int(s[3])
                 h, c0 = divmod(m * P, 256)
+                c0 += qm_raw[g, h][1]
                 copy_on(
                     CFG["eng"][s],
                     gm[m][:, g, :, :].rearrange("p (c i) t -> p c t i", i=4),
-                    qm_raw[g, h][:, :, c0 : c0 + P].rearrange("p t (c i) -> p c t i", i=4),
+                    qm_raw[g, h][0][:, :, c0 : c0 + P].rearrange("p t (c i) -> p c t i", i=4),
                 )
             elif s[:2] == "Qm":
                 codes = sb(s + "_codes", [P, G * P], U32)

@@ -33,7 +33,7 @@ def tile_attend_gat_lse_k_kernel(
         def sb(name, shape, dtype):
             return keep.tile(shape, dtype, name=name, align_bytes=64)
 
-        CFG = {"nw":3,"wG":True,"vf":True,"loads":["offs","vs0","vs1","vs2","vs3","delta","rw","d0","ks0","ks1","ks2","ks3","vw","lse","q0","kw","d1","q1a","q1b","qm00","qm10","qm01","qm11"],"order":["gvs","gks","cd0","Qd0","nd","gvw","W0","nl","cq0","gkw","Qq0","E0","cd1","Qd1","W1","cq1","Qq1","E1","M0","cm00","cm01","Qs0","Qm0","M1","Qs1","K0","cm10","cm11","Qm1","K1","cm20","cm21","Qm2","K2","cm30","cm31","Qm3","K3","X0","X1","X2","X3"],"eng":{"w00":"S","cm00":"V","w01":"S","cm10":"S","w02":"S","cm20":"S","w03":"S","cm30":"S","w10":"S","cm01":"V","w11":"S","cm11":"S","w12":"S","cm21":"S","w13":"S","cm31":"S","ek0":"S","ek1":"S","ek2":"S","ek3":"S"},"calls":{"Qq0":2,"Qq1":2,"Qd0":2,"Qd1":2},"ns":{"q0":0,"q1":0,"d0":3,"d1":0},"sp":{"E0":1,"W0":1,"E1":2,"W1":1},"mc":{"0":2,"1":2},"il":{"0":0,"1":0},"gate":{"d1":None,"q1a":"q0","q1b":"q0","qm00":"d1","qm10":"d1","qm01":"q1","qm11":"q1"}}
+        CFG = {"nw":3,"wG":False,"vf":True,"loads":["d0","offs","delta","vs0","vs1","vs2","vs3","vw","ks0","ks1","ks2","ks3","d1","q0a","rw","kw","q0b","lse","q1a","q1b","qm00","qm10","qm01","qm11"],"order":["cd0","Qd0","gvw","gvs","gks","cd1","Qd1","nd","W0","W1","gkw","cq0","nl","Qq0","cq1","Qq1","E0","E1","cm00","cm01","M0","Qs0","Qm0","M1","Qs1","K0","cm10","cm11","Qm1","K1","cm20","cm21","Qm2","K2","cm30","cm31","Qm3","K3","X0","X1","X2","X3"],"eng":{"w00":"S","cm00":"S","w01":"V","cm10":"S","w02":"S","cm20":"S","w03":"V","cm30":"S","w10":"S","cm01":"S","w11":"S","cm11":"S","w12":"S","cm21":"S","w13":"S","cm31":"S","ek0":"S","ek1":"S","ek2":"S","ek3":"S"},"calls":{"Qq0":4,"Qq1":2,"Qd0":2,"Qd1":2},"ns":{"d0":1,"d1":2,"q0":2,"q1":0},"sp":{"E0":2,"W0":1,"E1":2,"W1":1},"mc":{"0":2,"1":2},"il":{"0":0,"1":0},"gate":{},"vecG":False,"xs":True}
         offsets = keep.tile([P, N // 16], U16, name="offsets")
         pool_scales = {}
         for name in (("v", "k") if CFG["vf"] else ("k", "v")):
@@ -42,13 +42,6 @@ def tile_attend_gat_lse_k_kernel(
         warm = sb("warm", [P, 2], F32)
         nc.gpsimd.memset(warm[:, 0:1], 0.0)
         nc.scalar.activation(warm[:, 1:2], warm[:, 0:1], ACT.Exp)
-        windows = []
-        for w in range(CFG["nw"]):
-            windows.append(sb("window%d" % w, [P, T], F32))
-            if CFG["wG"] and w == CFG["nw"] - 1:
-                nc.gpsimd.memset(windows[w][:], 0.0)
-            else:
-                nc.vector.memset(windows[w][:], 0.0)
 
         used = {}
 
@@ -97,6 +90,16 @@ def tile_attend_gat_lse_k_kernel(
                 for quarter in range(width // P):
                     raw[x[0], c0 // P + quarter] = (x, tile, at + quarter * P)
 
+        if CFG.get("vecG"):
+            for x in ("delta", "rw", "lse"):
+                load(x)
+        windows = []
+        for w in range(CFG["nw"]):
+            windows.append(sb("window%d" % w, [P, T], F32))
+            if CFG["wG"] and w == CFG["nw"] - 1:
+                nc.gpsimd.memset(windows[w][:], 0.0)
+            else:
+                nc.vector.memset(windows[w][:], 0.0)
         for x in CFG["loads"]:
             if not CFG["gate"].get(x):
                 load(x)
@@ -265,10 +268,18 @@ def tile_attend_gat_lse_k_kernel(
                         stop=(g == G - 1),
                     )
                 made[s] = sb("dk%d" % m, [P, N], F32)
-                copy_on(CFG["eng"]["ek%d" % m], made[s][:], acc[:])
+                if m == 0 and CFG.get("xs"):
+                    nc.scalar.copy(made[s][:, 0:256], acc[:, 0:256])
+                    nc.scalar.copy(made[s][:, 256:512], acc[:, 256:512])
+                else:
+                    copy_on(CFG["eng"]["ek%d" % m], made[s][:], acc[:])
             elif s[0] == "X":
                 m = int(s[1])
                 window = windows[stores % len(windows)]
                 stores += 1
-                nc.vector.tensor_copy(window[:].indirect(offsets[:]), made["K%d" % m][:])
+                if m == 0 and CFG.get("xs"):
+                    nc.vector.tensor_copy(window[:].indirect(offsets[:, 0:16]), made["K0"][:, 0:256])
+                    nc.vector.tensor_copy(window[:].indirect(offsets[:, 16:32]), made["K0"][:, 256:512])
+                else:
+                    nc.vector.tensor_copy(window[:].indirect(offsets[:]), made["K%d" % m][:])
                 nc.sync.dma_start(out[m * P : (m + 1) * P, :], window[:])

@@ -11,15 +11,18 @@ I32 = mybir.dt.int32
 U32 = mybir.dt.uint32
 U16 = mybir.dt.uint16
 U8 = mybir.dt.uint8
-E4 = mybir.dt.float8_e4m3fn_x4
-E5 = mybir.dt.float8_e5m2_x4
+E4M3 = mybir.dt.float8_e4m3fn_x4
+E5M2 = mybir.dt.float8_e5m2_x4
 ALU = mybir.AluOpType
 ACT = mybir.ActivationFunctionType
 
 P = 128
 PACK = 4
-KP = P * PACK
-G = R // KP
+K_PASS = P * PACK
+PASSES = R // K_PASS
+D_TILES = D // P
+HALVES = (slice(0, N // 2), slice(N // 2, N))
+WINDOWS = 3
 
 
 def tile_attend_gat_lse_k_kernel(
@@ -30,256 +33,168 @@ def tile_attend_gat_lse_k_kernel(
         keep = ctx.enter_context(tc.tile_pool(name="keep", bufs=1))
         psum = ctx.enter_context(tc.psum_pool(name="psum", bufs=1))
 
-        def sb(name, shape, dtype):
+        def sbuf(name, shape, dtype):
             return keep.tile(shape, dtype, name=name, align_bytes=64)
 
-        CFG = {"nw":3,"wG":False,"vf":True,"loads":["d0","offs","delta","vs0","vs1","vs2","vs3","vw","ks0","ks1","ks2","ks3","d1","q0a","rw","kw","q0b","lse","q1a","q1b","qm00","qm10","qm01","qm11"],"order":["cd0","Qd0","gvw","gvs","gks","cd1","Qd1","nd","W0","W1","gkw","cq0","nl","Qq0","cq1","Qq1","E0","E1","cm00","cm01","M0","Qs0","Qm0","M1","Qs1","K0","cm10","cm11","Qm1","K1","cm20","cm21","Qm2","K2","cm30","cm31","Qm3","K3","X0","X1","X2","X3"],"eng":{"w00":"S","cm00":"S","w01":"V","cm10":"S","w02":"S","cm20":"S","w03":"V","cm30":"S","w10":"S","cm01":"S","w11":"S","cm11":"S","w12":"S","cm21":"S","w13":"S","cm31":"S","ek0":"S","ek1":"S","ek2":"S","ek3":"S"},"calls":{"Qq0":4,"Qq1":2,"Qd0":2,"Qd1":2},"ns":{"d0":1,"d1":2,"q0":2,"q1":0},"sp":{"E0":2,"W0":1,"E1":2,"W1":1},"mc":{"0":2,"1":2},"il":{"0":0,"1":0},"gate":{},"vecG":False,"xs":True}
-        offsets = keep.tile([P, N // 16], U16, name="offsets")
-        pool_scales = {}
-        for name in (("v", "k") if CFG["vf"] else ("k", "v")):
-            pool_scales[name] = sb(name + "_pool_scales", [P, T // 4], I32)
-            nc.gpsimd.memset(pool_scales[name][:], 0)
-        warm = sb("warm", [P, 2], F32)
+        def bank(index):
+            return psum.tile([P, N], F32, name="bank%d" % index, tag="bank%d" % index)
+
+        v_pool_scales = sbuf("v_pool_scales", [P, T // 4], I32)
+        nc.gpsimd.memset(v_pool_scales[:], 0)
+        k_pool_scales = sbuf("k_pool_scales", [P, T // 4], I32)
+        nc.gpsimd.memset(k_pool_scales[:], 0)
+
+        warm = sbuf("warm", [P, 2], F32)
         nc.gpsimd.memset(warm[:, 0:1], 0.0)
         nc.scalar.activation(warm[:, 1:2], warm[:, 0:1], ACT.Exp)
 
-        used = {}
+        windows = [sbuf("window%d" % w, [P, T], F32) for w in range(WINDOWS)]
+        for window in windows:
+            nc.vector.memset(window[:], 0.0)
 
-        def load_rows(name, src, c0, width):
-            y = CFG["gate"].get(name.replace("raw_", ""))
-            if y:
-                tile = raw[y[0], 4 * int(y[1])][1]
-                at = used.get(y, 0)
-                used[y] = at + width
-            else:
-                tile = sb(name, [P, PACK, width], F32)
-                at = 0
-            nc.sync.dma_start(tile[:, :, at : at + width], src.rearrange("(p j) c -> p j c", j=PACK)[:, :, c0 : c0 + width])
-            return tile, at
+        def load_rows(name, rows):
+            raw = sbuf(name, [P, PACK, rows.shape[1]], F32)
+            nc.sync.dma_start(raw[:], rows.rearrange("(p j) c -> p j c", j=PACK))
+            return raw
 
-        cols = {}
-        pool_words = {}
-        raw = {}
-        qm_raw = {}
-        def load(x):
-            if x == "offs":
-                nc.sync.dma_start(offsets[:], offs)
-            elif x in ("lse", "delta", "rw"):
-                src = {"lse": lse, "delta": delta, "rw": rw}[x]
-                cols[x] = sb(x + "_cols", [P, G, 2 * PACK], F32)[:, :, 0:PACK]
-                (nc.gpsimd if CFG.get("vecG") else nc.sync).dma_start(cols[x], src[0].rearrange("(g p t) o -> p g (t o)", g=G, t=PACK))
-            elif x in ("kw", "vw"):
-                pool_words[x[0]] = sb(x + "_pool_words", [P, T], I32)
-                src = k_words if x == "kw" else v_words
-                nc.sync.dma_start(pool_words[x[0]][:], src[0].rearrange("p t j -> p (t j)").bitcast(I32))
-            elif x[:2] in ("ks", "vs"):
-                r = int(x[2])
-                src = k_scales if x[0] == "k" else v_scales
-                nc.sync.dma_start(pool_scales[x[0]][r:P:32, :], src[0, r:16:4, :].bitcast(I32))
-            elif x[:2] == "qm":
-                g, h = int(x[2]), int(x[3])
-                qm_raw[g, h] = load_rows(x, qm[0, g * KP : (g + 1) * KP, :], h * 256, 256)
-            else:
-                width = {1: 1024, 2: 512, 3: 256}[len(x)]
-                c0 = 0
-                if len(x) > 1:
-                    c0 += int(x[1]) * KP
-                if len(x) > 2:
-                    c0 += 256 * (x[2] == "b")
-                tile, at = load_rows("raw_" + x, qT[0] if x[0] == "q" else doT[0], c0, width)
-                for quarter in range(width // P):
-                    raw[x[0], c0 // P + quarter] = (x, tile, at + quarter * P)
+        def load_per_query(name, values):
+            columns = sbuf(name, [P, PASSES, 2 * PACK], F32)[:, :, 0:PACK]
+            nc.sync.dma_start(columns, values[0].rearrange("(g p t) o -> p g (t o)", g=PASSES, t=PACK))
+            return columns
 
-        if CFG.get("vecG"):
-            for x in ("delta", "rw", "lse"):
-                load(x)
-        windows = []
-        for w in range(CFG["nw"]):
-            windows.append(sb("window%d" % w, [P, T], F32))
-            if CFG["wG"] and w == CFG["nw"] - 1:
-                nc.gpsimd.memset(windows[w][:], 0.0)
-            else:
-                nc.vector.memset(windows[w][:], 0.0)
-        for x in CFG["loads"]:
-            if not CFG["gate"].get(x):
-                load(x)
+        def load_pool_words(name, words):
+            pool_words = sbuf(name, [P, T], I32)
+            nc.sync.dma_start(pool_words[:], words[0].rearrange("p t j -> p (t j)").bitcast(I32))
+            return pool_words
 
-        def flat(tile):
-            return tile[:].rearrange("p a b c -> p (a b c)")
+        def load_pool_scales(pool_scales, scales):
+            for row in range(4):
+                nc.sync.dma_start(pool_scales[row:P:32, :], scales[0, row:16:4, :].bitcast(I32))
 
-        def bank(b):
-            return psum.tile([P, N], F32, name="bank%d" % b, tag="bank%d" % b)
+        def queries(g):
+            return slice(g * K_PASS, (g + 1) * K_PASS)
 
-        def copy_on(engine, dst, src):
-            if engine == "S":
-                nc.scalar.copy(dst, src)
-            else:
-                nc.vector.tensor_copy(dst, src)
+        do_raw, q_raw = [None] * PASSES, [None] * PASSES
+        do_raw[0] = load_rows("do_raw0", doT[0, :, queries(0)])
+        offsets = keep.tile([P, N // 16], U16, name="offsets")
+        nc.sync.dma_start(offsets[:], offs)
+        delta_q = load_per_query("delta_q", delta)
+        load_pool_scales(v_pool_scales, v_scales)
+        v_pool_words = load_pool_words("v_pool_words", v_words)
+        load_pool_scales(k_pool_scales, k_scales)
+        lse_q = load_per_query("lse_q", lse)
+        do_raw[1] = load_rows("do_raw1", doT[0, :, queries(1)])
+        rw_q = load_per_query("rw_q", rw)
+        q_raw[0] = load_rows("q_raw0", qT[0, :, queries(0)])
+        k_pool_words = load_pool_words("k_pool_words", k_words)
+        q_raw[1] = load_rows("q_raw1", qT[0, :, queries(1)])
+        qm_raw = [load_rows("qm_raw%d" % g, qm[0, queries(g), :]) for g in range(PASSES)]
 
-        def quantize(name, grouped, fmt, calls):
-            codes = sb(name + "_codes", [P, KP], U32)
-            scales = sb(name + "_scales", [P, KP], U8)
-            w = KP // calls
-            for c in range(calls):
-                nc.vector.quantize_mx(
-                    out=codes[:, c * w : (c + 1) * w].bitcast(fmt),
-                    scales=scales[:, c * w : (c + 1) * w],
-                    in_=grouped[:, PACK * c * w : PACK * (c + 1) * w],
-                )
-            return codes, scales
+        def gather(name, window, dtype):
+            listed = sbuf(name, [P, N], dtype)
+            nc.vector.tensor_copy(listed[:], window[:].bitcast(dtype).indirect(offsets[:]))
+            return listed
 
-        def product(b, stat, t, fmt, pool):
-            acc = bank(b)
+        def mx_tiles(name, width):
+            return sbuf(name + "_codes", [P, width], U32), sbuf(name + "_scales", [P, width], U8)
+
+        def quantize(mx, columns, grouped, fmt):
+            nc.vector.quantize_mx(out=mx[0][:, columns].bitcast(fmt), scales=mx[1][:, columns], in_=grouped)
+
+        def quantize_by_query(name, raw, fmt):
+            grouped = sbuf(name + "_grouped", [P, PACK, P, PACK], BF16)
+            nc.vector.tensor_copy(
+                grouped[:].rearrange("p t m j -> p m j t"), raw[:].rearrange("p j (m t) -> p m j t", t=PACK)
+            )
+            mx = mx_tiles(name, K_PASS)
+            for t in range(PACK):
+                quantize(mx, slice(t * P, (t + 1) * P), grouped[:, t, :, :].rearrange("p m j -> p (m j)"), fmt)
+            return mx
+
+        def multiply(acc, stationary, run, stationary_fmt, moving, moving_fmt, start, stop):
+            columns = slice(run * P, (run + 1) * P)
             nc.tensor.matmul_mx(
                 out=acc[:],
-                lhsT=stat[0][:, t * P : (t + 1) * P].bitcast(fmt),
-                lhsT_scale=stat[1][:, t * P : (t + 1) * P],
-                rhs=made["g" + pool + "w"][:].bitcast(E4),
-                rhs_scale=made["g" + pool + "s"][:],
-                start=True,
-                stop=True,
+                lhsT=stationary[0][:, columns].bitcast(stationary_fmt),
+                lhsT_scale=stationary[1][:, columns],
+                rhs=moving[0][:].bitcast(moving_fmt),
+                rhs_scale=moving[1][:],
+                start=start,
+                stop=stop,
             )
-            return acc
 
-        made = {}
-        p_t = [sb("p%d" % g, [P, PACK, N], F32) for g in range(G)]
-        w_t = [sb("w%d" % g, [P, PACK, N], F32) for g in range(G)]
-        gm = [sb("gm%d" % m, [P, G, P, PACK], BF16) for m in range(4)]
-        stores = 0
-        for s in CFG["order"]:
-            if s == "nl":
-                made[s] = sb("neg_lse", [P, G, PACK], F32)
-                nc.vector.tensor_scalar(made[s][:], cols["lse"], -1.0, None, ALU.mult)
-            elif s == "nd":
-                made[s] = sb("neg_delta_rw", [P, G, PACK], F32)
-                nc.vector.scalar_tensor_tensor(made[s][:], cols["delta"], -1.0, cols["rw"], ALU.mult, ALU.mult)
-            elif s in ("gks", "gvs"):
-                made[s] = sb(s, [P, N], U8)
-                nc.vector.tensor_copy(made[s][:], pool_scales[s[1]][:].bitcast(U8).indirect(offsets[:]))
-            elif s in ("gkw", "gvw"):
-                made[s] = sb(s, [P, N], U32)
-                nc.vector.tensor_copy(made[s][:], pool_words[s[1]][:].bitcast(U32).indirect(offsets[:]))
-            elif s[0] == "c" and s[1] in "qd":
-                g = int(s[2])
-                grouped = sb(s, [P, PACK, P, PACK], BF16)
-                made[s] = grouped
-                pieces = []
-                for i in range(4):
-                    e = "S" if i < CFG["ns"][s[1:]] else "V"
-                    x, tile, c0 = raw[s[1], 4 * g + i]
-                    if pieces and pieces[-1][0] == e and pieces[-1][1] == x:
-                        pieces[-1][4] += P
-                    else:
-                        pieces.append([e, x, tile, c0, P, i])
-                for e, x, tile, c0, width, i in pieces:
-                    copy_on(
-                        e,
-                        grouped[:, :, 32 * i : 32 * i + width // PACK, :].rearrange("p t m j -> p m j t"),
-                        tile[:, :, c0 : c0 + width].rearrange("p j (m t) -> p m j t", t=PACK),
-                    )
-                for x in CFG["loads"]:
-                    if CFG["gate"].get(x) == s[1:]:
-                        load(x)
-            elif s[0] == "Q" and s[1] in "qd":
-                made[s] = quantize(s, flat(made["c" + s[1:]]), E4 if s[1] == "q" else E5, CFG["calls"][s])
-            elif s[0] in "EW":
-                g = int(s[1])
-                sp = CFG["sp"][s]
-                accs = []
-                for h in range(sp):
-                    c = slice(h * N // sp, (h + 1) * N // sp)
-                    for t in range(PACK):
-                        if h == 0:
-                            if s[0] == "E":
-                                accs.append(product(t, made["Qq%d" % g], t, E4, "k"))
-                            else:
-                                accs.append(product(PACK + t, made["Qd%d" % g], t, E5, "v"))
-                        acc = accs[t]
-                        if s[0] == "E":
-                            nc.scalar.activation(p_t[g][:, t, c], acc[:, c], ACT.Exp, bias=made["nl"][:, g, t : t + 1])
-                        elif CFG["eng"]["w%d%d" % (g, t)] == "V":
-                            nc.vector.tensor_scalar(
-                                w_t[g][:, t, c], acc[:, c], cols["delta"][:, g, t : t + 1], cols["rw"][:, g, t : t + 1],
-                                ALU.subtract, ALU.mult,
-                            )
-                        else:
-                            nc.scalar.activation(
-                                w_t[g][:, t, c], acc[:, c], ACT.Identity,
-                                bias=made["nd"][:, g, t : t + 1], scale=cols["rw"][:, g, t : t + 1],
-                            )
-            elif s[0] == "M" or s[:2] == "Qs":
-                g = int(s[-1])
-                mc = CFG["mc"][s[-1]]
-                wide = N // mc
-                if s[0] == "M":
-                    made[s] = sb("ds%d" % g, [P, N, PACK], BF16)
-                    made["Qs%d" % g] = (sb("ds_codes%d" % g, [P, N], U32), sb("ds_scales%d" % g, [P, N], U8))
-                ds = made["M%d" % g]
-                todo = []
-                if s[0] == "M":
-                    for h in range(mc):
-                        todo.append(("m", h))
-                        if CFG["il"][s[-1]] and h > 0:
-                            todo.append(("q", h - 1))
-                else:
-                    for h in range(mc - 1 if CFG["il"][s[-1]] else 0, mc):
-                        todo.append(("q", h))
-                for kind, h in todo:
-                    c = slice(h * wide, (h + 1) * wide)
-                    if kind == "m":
-                        nc.vector.tensor_tensor(
-                            ds[:, c, :].rearrange("p (c i) t -> p c t i", i=4),
-                            p_t[g][:, :, c].rearrange("p t (c i) -> p c t i", i=4),
-                            w_t[g][:, :, c].rearrange("p t (c i) -> p c t i", i=4),
-                            ALU.mult,
-                        )
-                    else:
-                        nc.vector.quantize_mx(
-                            out=made["Qs%d" % g][0][:, c].bitcast(E5),
-                            scales=made["Qs%d" % g][1][:, c],
-                            in_=ds[:, c, :].rearrange("p i t -> p (i t)"),
-                        )
-            elif s[:2] == "cm":
-                m, g = int(s[2]), int(s[3])
-                h, c0 = divmod(m * P, 256)
-                c0 += qm_raw[g, h][1]
-                copy_on(
-                    CFG["eng"][s],
-                    gm[m][:, g, :, :].rearrange("p (c i) t -> p c t i", i=4),
-                    qm_raw[g, h][0][:, :, c0 : c0 + P].rearrange("p t (c i) -> p c t i", i=4),
+        values = (gather("v_codes", v_pool_words, U32), gather("v_scales", v_pool_scales, U8))
+        neg_delta_rw = sbuf("neg_delta_rw", [P, PASSES, PACK], F32)
+        nc.vector.scalar_tensor_tensor(neg_delta_rw[:], delta_q, -1.0, rw_q, ALU.mult, ALU.mult)
+        gated = [sbuf("gated%d" % g, [P, PACK, N], F32) for g in range(PASSES)]
+        for g in range(PASSES):
+            do_mx = quantize_by_query("do%d" % g, do_raw[g], E5M2)
+            for t in range(PACK):
+                dp = bank(PACK + t)
+                multiply(dp, do_mx, t, E5M2, values, E4M3, True, True)
+                nc.scalar.activation(
+                    gated[g][:, t, :], dp[:], ACT.Identity,
+                    bias=neg_delta_rw[:, g, t : t + 1], scale=rw_q[:, g, t : t + 1],
                 )
-            elif s[:2] == "Qm":
-                codes = sb(s + "_codes", [P, G * P], U32)
-                scales = sb(s + "_scales", [P, G * P], U8)
-                nc.vector.quantize_mx(out=codes[:].bitcast(E4), scales=scales[:], in_=flat(gm[int(s[2])]))
-                made[s] = (codes, scales)
-            elif s[0] == "K":
-                m = int(s[1])
-                codes, scales = made["Qm%d" % m]
-                acc = bank(m)
-                for g in range(G):
-                    nc.tensor.matmul_mx(
-                        out=acc[:],
-                        lhsT=codes[:, g * P : (g + 1) * P].bitcast(E4),
-                        lhsT_scale=scales[:, g * P : (g + 1) * P],
-                        rhs=made["Qs%d" % g][0][:].bitcast(E5),
-                        rhs_scale=made["Qs%d" % g][1][:],
-                        start=(g == 0),
-                        stop=(g == G - 1),
+
+        k_listed_scales = gather("k_scales", k_pool_scales, U8)
+        keys = (gather("k_codes", k_pool_words, U32), k_listed_scales)
+        neg_lse = sbuf("neg_lse", [P, PASSES, PACK], F32)
+        nc.vector.tensor_scalar(neg_lse[:], lse_q, -1.0, None, ALU.mult)
+        weights = [sbuf("weights%d" % g, [P, PACK, N], F32) for g in range(PASSES)]
+        for g in range(PASSES):
+            q_mx = quantize_by_query("q%d" % g, q_raw[g], E4M3)
+            scores = []
+            for half in HALVES:
+                for t in range(PACK):
+                    if half.start == 0:
+                        scores.append(bank(t))
+                        multiply(scores[t], q_mx, t, E4M3, keys, E4M3, True, True)
+                    nc.scalar.activation(
+                        weights[g][:, t, half], scores[t][:, half], ACT.Exp, bias=neg_lse[:, g, t : t + 1]
                     )
-                made[s] = sb("dk%d" % m, [P, N], F32)
-                if m == 0 and CFG.get("xs"):
-                    nc.scalar.copy(made[s][:, 0:256], acc[:, 0:256])
-                    nc.scalar.copy(made[s][:, 256:512], acc[:, 256:512])
-                else:
-                    copy_on(CFG["eng"]["ek%d" % m], made[s][:], acc[:])
-            elif s[0] == "X":
-                m = int(s[1])
-                window = windows[stores % len(windows)]
-                stores += 1
-                if m == 0 and CFG.get("xs"):
-                    nc.vector.tensor_copy(window[:].indirect(offsets[:, 0:16]), made["K0"][:, 0:256])
-                    nc.vector.tensor_copy(window[:].indirect(offsets[:, 16:32]), made["K0"][:, 256:512])
-                else:
-                    nc.vector.tensor_copy(window[:].indirect(offsets[:]), made["K%d" % m][:])
-                nc.sync.dma_start(out[m * P : (m + 1) * P, :], window[:])
+
+        def quantize_qm(m):
+            grouped = sbuf("qm_grouped%d" % m, [P, PASSES, P, PACK], BF16)
+            mx = mx_tiles("qm%d" % m, PASSES * P)
+            for g in range(PASSES):
+                nc.scalar.copy(
+                    grouped[:, g, :, :].rearrange("p (c i) t -> p c t i", i=4),
+                    qm_raw[g][:, :, m * P : (m + 1) * P].rearrange("p t (c i) -> p c t i", i=4),
+                )
+                quantize(mx, slice(g * P, (g + 1) * P), grouped[:, g, :, :].rearrange("p d t -> p (d t)"), E4M3)
+            return mx
+
+        ds_mx, qm_mx = [], []
+        for g in range(PASSES):
+            ds = sbuf("ds%d" % g, [P, N, PACK], BF16)
+            ds_mx.append(mx_tiles("ds%d" % g, N))
+            for half in HALVES:
+                nc.vector.tensor_tensor(
+                    ds[:, half, :].rearrange("p (c i) t -> p c t i", i=2),
+                    weights[g][:, :, half].rearrange("p t (c i) -> p c t i", i=2),
+                    gated[g][:, :, half].rearrange("p t (c i) -> p c t i", i=2),
+                    ALU.mult,
+                )
+            if g == PASSES - 1:
+                qm_mx.append(quantize_qm(0))
+            for half in HALVES:
+                quantize(ds_mx[g], half, ds[:, half, :].rearrange("p i t -> p (i t)"), E5M2)
+
+        dk = []
+        for m in range(D_TILES):
+            if m > 0:
+                qm_mx.append(quantize_qm(m))
+            acc = bank(m)
+            for g in range(PASSES):
+                multiply(acc, qm_mx[m], g, E4M3, ds_mx[g], E5M2, g == 0, g == PASSES - 1)
+            dk.append(sbuf("dk%d" % m, [P, N], F32))
+            for part in HALVES if m == 0 else (slice(0, N),):
+                nc.scalar.copy(dk[m][:, part], acc[:, part])
+
+        for m in range(D_TILES):
+            window = windows[m % WINDOWS]
+            for part in HALVES if m == 0 else (slice(0, N),):
+                entries = offsets[:, part.start // 16 : part.stop // 16]
+                nc.vector.tensor_copy(window[:].indirect(entries), dk[m][:, part])
+            nc.sync.dma_start(out[m * P : (m + 1) * P, :], window[:])

@@ -33,8 +33,8 @@ def tile_attend_gat_lse_k_kernel(
         keep = ctx.enter_context(tc.tile_pool(name="keep", bufs=1))
         psum = ctx.enter_context(tc.psum_pool(name="psum", bufs=1))
 
-        def sbuf(name, shape, dtype):
-            return keep.tile(shape, dtype, name=name, align_bytes=64)
+        def sbuf(name, shape, dtype, tag=None):
+            return keep.tile(shape, dtype, name=name, tag=tag or name, align_bytes=64)
 
         def bank(index):
             return psum.tile([P, N], F32, name="bank%d" % index, tag="bank%d" % index)
@@ -88,7 +88,8 @@ def tile_attend_gat_lse_k_kernel(
         q_raw[0] = load_rows("q_raw0", qT[0, :, queries(0)])
         k_pool_words = load_pool_words("k_pool_words", k_words)
         q_raw[1] = load_rows("q_raw1", qT[0, :, queries(1)])
-        qm_raw = [load_rows("qm_raw%d" % g, qm[0, queries(g), :]) for g in range(PASSES)]
+        qm_raw_first = [load_rows("qm_raw_first%d" % g, qm[0, queries(g), 0:P]) for g in range(PASSES)]
+        qm_raw_later = [load_rows("qm_raw_later%d" % g, qm[0, queries(g), P:D]) for g in range(PASSES)]
 
         def gather(name, window, dtype):
             listed = sbuf(name, [P, N], dtype)
@@ -101,11 +102,15 @@ def tile_attend_gat_lse_k_kernel(
         def quantize(mx, columns, grouped, fmt):
             nc.vector.quantize_mx(out=mx[0][:, columns].bitcast(fmt), scales=mx[1][:, columns], in_=grouped)
 
-        def quantize_by_query(name, raw, fmt):
+        def quantize_by_query(name, raw, fmt, copies):
             grouped = sbuf(name + "_grouped", [P, PACK, P, PACK], BF16)
-            nc.vector.tensor_copy(
-                grouped[:].rearrange("p t m j -> p m j t"), raw[:].rearrange("p j (m t) -> p m j t", t=PACK)
-            )
+            share = P // len(copies)
+            for index, copy in enumerate(copies):
+                m_range = slice(index * share, (index + 1) * share)
+                copy(
+                    grouped[:].rearrange("p t m j -> p m j t")[:, m_range],
+                    raw[:].rearrange("p j (m t) -> p m j t", t=PACK)[:, m_range],
+                )
             mx = mx_tiles(name, K_PASS)
             for t in range(PACK):
                 quantize(mx, slice(t * P, (t + 1) * P), grouped[:, t, :, :].rearrange("p m j -> p (m j)"), fmt)
@@ -128,7 +133,7 @@ def tile_attend_gat_lse_k_kernel(
         nc.vector.scalar_tensor_tensor(neg_delta_rw[:], delta_q, -1.0, rw_q, ALU.mult, ALU.mult)
         gated = [sbuf("gated%d" % g, [P, PACK, N], F32) for g in range(PASSES)]
         for g in range(PASSES):
-            do_mx = quantize_by_query("do%d" % g, do_raw[g], E5M2)
+            do_mx = quantize_by_query("do%d" % g, do_raw[g], E5M2, (nc.scalar.copy, nc.vector.tensor_copy))
             for t in range(PACK):
                 dp = bank(PACK + t)
                 multiply(dp, do_mx, t, E5M2, values, E4M3, True, True)
@@ -143,7 +148,7 @@ def tile_attend_gat_lse_k_kernel(
         nc.vector.tensor_scalar(neg_lse[:], lse_q, -1.0, None, ALU.mult)
         weights = [sbuf("weights%d" % g, [P, PACK, N], F32) for g in range(PASSES)]
         for g in range(PASSES):
-            q_mx = quantize_by_query("q%d" % g, q_raw[g], E4M3)
+            q_mx = quantize_by_query("q%d" % g, q_raw[g], E4M3, (nc.vector.tensor_copy,))
             scores = []
             for half in HALVES:
                 for t in range(PACK):
@@ -154,18 +159,18 @@ def tile_attend_gat_lse_k_kernel(
                         weights[g][:, t, half], scores[t][:, half], ACT.Exp, bias=neg_lse[:, g, t : t + 1]
                     )
 
-        def quantize_qm(m):
+        def quantize_qm(m, raw, raw_block, mx):
             grouped = sbuf("qm_grouped%d" % m, [P, PASSES, P, PACK], BF16)
-            mx = mx_tiles("qm%d" % m, PASSES * P)
             for g in range(PASSES):
                 nc.scalar.copy(
                     grouped[:, g, :, :].rearrange("p (c i) t -> p c t i", i=4),
-                    qm_raw[g][:, :, m * P : (m + 1) * P].rearrange("p t (c i) -> p c t i", i=4),
+                    raw[g][:, :, raw_block * P : (raw_block + 1) * P].rearrange("p t (c i) -> p c t i", i=4),
                 )
-                quantize(mx, slice(g * P, (g + 1) * P), grouped[:, g, :, :].rearrange("p d t -> p (d t)"), E4M3)
-            return mx
+                run = PASSES * raw_block + g
+                quantize(mx, slice(run * P, (run + 1) * P), grouped[:, g, :, :].rearrange("p d t -> p (d t)"), E4M3)
 
-        ds_mx, qm_mx = [], []
+        ds_mx = []
+        qm_first = mx_tiles("qm_first", PASSES * P)
         for g in range(PASSES):
             ds = sbuf("ds%d" % g, [P, N, PACK], BF16)
             ds_mx.append(mx_tiles("ds%d" % g, N))
@@ -177,17 +182,23 @@ def tile_attend_gat_lse_k_kernel(
                     ALU.mult,
                 )
             if g == PASSES - 1:
-                qm_mx.append(quantize_qm(0))
+                quantize_qm(0, qm_raw_first, 0, qm_first)
             for half in HALVES:
                 quantize(ds_mx[g], half, ds[:, half, :].rearrange("p i t -> p (i t)"), E5M2)
 
+        later_width = (D_TILES - 1) * PASSES * P
+        qm_later = (
+            sbuf("qm_later_codes", [P, later_width], U32, tag="ds%d" % (PASSES - 1)),
+            sbuf("qm_later_scales", [P, later_width], U8),
+        )
         dk = []
         for m in range(D_TILES):
+            qm_mx, first_run = (qm_first, 0) if m == 0 else (qm_later, (m - 1) * PASSES)
             if m > 0:
-                qm_mx.append(quantize_qm(m))
+                quantize_qm(m, qm_raw_later, m - 1, qm_later)
             acc = bank(m)
             for g in range(PASSES):
-                multiply(acc, qm_mx[m], g, E4M3, ds_mx[g], E5M2, g == 0, g == PASSES - 1)
+                multiply(acc, qm_mx, first_run + g, E4M3, ds_mx[g], E5M2, g == 0, g == PASSES - 1)
             dk.append(sbuf("dk%d" % m, [P, N], F32))
             for part in HALVES if m == 0 else (slice(0, N),):
                 nc.scalar.copy(dk[m][:, part], acc[:, part])

@@ -22,6 +22,7 @@ K_PASS = P * PACK
 PASSES = R // K_PASS
 D_TILES = D // P
 HALVES = (slice(0, N // 2), slice(N // 2, N))
+QUARTERS = tuple(slice(c * N // 4, (c + 1) * N // 4) for c in range(4))
 WINDOWS = 3
 
 
@@ -42,7 +43,7 @@ def tile_attend_gat_lse_k_kernel(
         v_pool_scales = sbuf("v_pool_scales", [P, T // 4], I32)
         nc.gpsimd.memset(v_pool_scales[:], 0)
         k_pool_scales = sbuf("k_pool_scales", [P, T // 4], I32)
-        nc.gpsimd.memset(k_pool_scales[:], 0)
+        nc.vector.memset(k_pool_scales[:], 0)
 
         warm = sbuf("warm", [P, 2], F32)
         nc.gpsimd.memset(warm[:, 0:1], 0.0)
@@ -50,11 +51,13 @@ def tile_attend_gat_lse_k_kernel(
 
         windows = [sbuf("window%d" % w, [P, T], F32) for w in range(WINDOWS)]
         for window in windows:
-            nc.vector.memset(window[:], 0.0)
+            nc.gpsimd.memset(window[:], 0.0)
 
-        def load_rows(name, rows):
+        def load_rows(name, rows, pieces=1):
             raw = sbuf(name, [P, PACK, rows.shape[1]], F32)
-            nc.sync.dma_start(raw[:], rows.rearrange("(p j) c -> p j c", j=PACK))
+            step = PACK // pieces
+            for j in range(0, PACK, step):
+                nc.sync.dma_start(raw[:, j : j + step, :], rows.rearrange("(p j) c -> p j c", j=PACK)[:, j : j + step, :])
             return raw
 
         def load_per_query(name, values):
@@ -67,26 +70,27 @@ def tile_attend_gat_lse_k_kernel(
             nc.sync.dma_start(pool_words[:], words[0].rearrange("p t j -> p (t j)").bitcast(I32))
             return pool_words
 
-        def load_pool_scales(pool_scales, scales):
-            for row in range(4):
+        def load_pool_scales(pool_scales, scales, rows):
+            for row in rows:
                 nc.sync.dma_start(pool_scales[row:P:32, :], scales[0, row:16:4, :].bitcast(I32))
 
         def queries(g):
             return slice(g * K_PASS, (g + 1) * K_PASS)
 
         do_raw, q_raw = [None] * PASSES, [None] * PASSES
-        do_raw[0] = load_rows("do_raw0", doT[0, :, queries(0)])
         offsets = keep.tile([P, N // 16], U16, name="offsets")
         nc.sync.dma_start(offsets[:], offs)
         delta_q = load_per_query("delta_q", delta)
-        load_pool_scales(v_pool_scales, v_scales)
-        v_pool_words = load_pool_words("v_pool_words", v_words)
-        load_pool_scales(k_pool_scales, k_scales)
-        lse_q = load_per_query("lse_q", lse)
-        do_raw[1] = load_rows("do_raw1", doT[0, :, queries(1)])
         rw_q = load_per_query("rw_q", rw)
+        lse_q = load_per_query("lse_q", lse)
+        do_raw[0] = load_rows("do_raw0", doT[0, :, queries(0)], pieces=2)
+        load_pool_scales(v_pool_scales, v_scales, range(4))
+        load_pool_scales(k_pool_scales, k_scales, range(2))
+        v_pool_words = load_pool_words("v_pool_words", v_words)
+        load_pool_scales(k_pool_scales, k_scales, range(2, 4))
         q_raw[0] = load_rows("q_raw0", qT[0, :, queries(0)])
         k_pool_words = load_pool_words("k_pool_words", k_words)
+        do_raw[1] = load_rows("do_raw1", doT[0, :, queries(1)])
         q_raw[1] = load_rows("q_raw1", qT[0, :, queries(1)])
         qm_raw_first = [load_rows("qm_raw_first%d" % g, qm[0, queries(g), 0:P]) for g in range(PASSES)]
         qm_raw_later = [load_rows("qm_raw_later%d" % g, qm[0, queries(g), P:D]) for g in range(PASSES)]
@@ -96,22 +100,23 @@ def tile_attend_gat_lse_k_kernel(
             nc.vector.tensor_copy(listed[:], window[:].bitcast(dtype).indirect(offsets[:]))
             return listed
 
-        def mx_tiles(name, width):
-            return sbuf(name + "_codes", [P, width], U32), sbuf(name + "_scales", [P, width], U8)
+        def mx_tiles(name, width, tag=None):
+            return sbuf(name + "_codes", [P, width], U32, tag=tag), sbuf(name + "_scales", [P, width], U8)
 
         def quantize(mx, columns, grouped, fmt):
             nc.vector.quantize_mx(out=mx[0][:, columns].bitcast(fmt), scales=mx[1][:, columns], in_=grouped)
 
-        def quantize_by_query(name, raw, fmt, copies):
-            grouped = sbuf(name + "_grouped", [P, PACK, P, PACK], BF16)
-            share = P // len(copies)
-            for index, copy in enumerate(copies):
-                m_range = slice(index * share, (index + 1) * share)
+        def round_by_query(name, raw, shares, tag=None):
+            grouped = sbuf(name + "_grouped", [P, PACK, P, PACK], BF16, tag=tag)
+            for copy, first, last in shares:
                 copy(
-                    grouped[:].rearrange("p t m j -> p m j t")[:, m_range],
-                    raw[:].rearrange("p j (m t) -> p m j t", t=PACK)[:, m_range],
+                    grouped[:].rearrange("p t m j -> p m j t")[:, first:last],
+                    raw[:].rearrange("p j (m t) -> p m j t", t=PACK)[:, first:last],
                 )
-            mx = mx_tiles(name, K_PASS)
+            return grouped
+
+        def quantize_by_query(name, grouped, fmt, tag=None):
+            mx = mx_tiles(name, K_PASS, tag)
             for t in range(PACK):
                 quantize(mx, slice(t * P, (t + 1) * P), grouped[:, t, :, :].rearrange("p m j -> p (m j)"), fmt)
             return mx
@@ -128,12 +133,11 @@ def tile_attend_gat_lse_k_kernel(
                 stop=stop,
             )
 
-        values = (gather("v_codes", v_pool_words, U32), gather("v_scales", v_pool_scales, U8))
-        neg_delta_rw = sbuf("neg_delta_rw", [P, PASSES, PACK], F32)
-        nc.vector.scalar_tensor_tensor(neg_delta_rw[:], delta_q, -1.0, rw_q, ALU.mult, ALU.mult)
         gated = [sbuf("gated%d" % g, [P, PACK, N], F32) for g in range(PASSES)]
-        for g in range(PASSES):
-            do_mx = quantize_by_query("do%d" % g, do_raw[g], E5M2, (nc.scalar.copy, nc.vector.tensor_copy))
+        weights = [sbuf("weights%d" % g, [P, PACK, N], F32) for g in range(PASSES)]
+        ds_mx = [mx_tiles("ds%d" % g, N) for g in range(PASSES)]
+
+        def gate(g, do_mx):
             for t in range(PACK):
                 dp = bank(PACK + t)
                 multiply(dp, do_mx, t, E5M2, values, E4M3, True, True)
@@ -142,13 +146,7 @@ def tile_attend_gat_lse_k_kernel(
                     bias=neg_delta_rw[:, g, t : t + 1], scale=rw_q[:, g, t : t + 1],
                 )
 
-        k_listed_scales = gather("k_scales", k_pool_scales, U8)
-        keys = (gather("k_codes", k_pool_words, U32), k_listed_scales)
-        neg_lse = sbuf("neg_lse", [P, PASSES, PACK], F32)
-        nc.vector.tensor_scalar(neg_lse[:], lse_q, -1.0, None, ALU.mult)
-        weights = [sbuf("weights%d" % g, [P, PACK, N], F32) for g in range(PASSES)]
-        for g in range(PASSES):
-            q_mx = quantize_by_query("q%d" % g, q_raw[g], E4M3, (nc.vector.tensor_copy,))
+        def weigh(g, q_mx):
             scores = []
             for half in HALVES:
                 for t in range(PACK):
@@ -158,6 +156,19 @@ def tile_attend_gat_lse_k_kernel(
                     nc.scalar.activation(
                         weights[g][:, t, half], scores[t][:, half], ACT.Exp, bias=neg_lse[:, g, t : t + 1]
                     )
+
+        def ds_product(g, part, tag=None):
+            ds = sbuf("ds%d_%d" % (g, part.start), [P, part.stop - part.start, PACK], BF16, tag=tag)
+            nc.vector.tensor_tensor(
+                ds[:].rearrange("p (c i) t -> p c t i", i=2),
+                weights[g][:, :, part].rearrange("p t (c i) -> p c t i", i=2),
+                gated[g][:, :, part].rearrange("p t (c i) -> p c t i", i=2),
+                ALU.mult,
+            )
+            return ds
+
+        def ds_quantize(g, part, ds):
+            quantize(ds_mx[g], part, ds[:].rearrange("p i t -> p (i t)"), E5M2)
 
         def quantize_qm(m, raw, raw_block, mx):
             grouped = sbuf("qm_grouped%d" % m, [P, PASSES, P, PACK], BF16)
@@ -169,26 +180,40 @@ def tile_attend_gat_lse_k_kernel(
                 run = PASSES * raw_block + g
                 quantize(mx, slice(run * P, (run + 1) * P), grouped[:, g, :, :].rearrange("p d t -> p (d t)"), E4M3)
 
-        ds_mx = []
+        by_scalar, by_vector = nc.scalar.copy, nc.vector.tensor_copy
+
+        do_grouped = round_by_query("do0", do_raw[0], ((by_scalar, 0, P // 2), (by_vector, P // 2, P)))
+        v_listed_scales = gather("v_scales", v_pool_scales, U8)
+        do_mx = quantize_by_query("do0", do_grouped, E5M2, tag="v_pool_scales")
+        values = (gather("v_codes", v_pool_words, U32), v_listed_scales)
+        neg_delta_rw = sbuf("neg_delta_rw", [P, PASSES, PACK], F32)
+        nc.vector.scalar_tensor_tensor(neg_delta_rw[:], delta_q, -1.0, rw_q, ALU.mult, ALU.mult)
+        neg_lse = sbuf("neg_lse", [P, PASSES, PACK], F32)
+        nc.scalar.mul(neg_lse[:], lse_q, -1.0)
+        gate(0, do_mx)
+        k_listed_scales = gather("k_scales", k_pool_scales, U8)
+        q_mx = quantize_by_query("q0", round_by_query("q0", q_raw[0], ((by_vector, 0, P),), tag="k_pool_scales"), E4M3)
+        keys = (gather("k_codes", k_pool_words, U32), k_listed_scales)
+        weigh(0, q_mx)
+
+        do_mx = quantize_by_query("do1", round_by_query("do1", do_raw[1], ((by_vector, 0, P),)), E5M2)
+        gate(1, do_mx)
+        ds_parts = [ds_product(0, QUARTERS[0], tag="do1_grouped")]
+        q_mx = quantize_by_query("q1", round_by_query("q1", q_raw[1], ((by_vector, 0, P),)), E4M3)
+        weigh(1, q_mx)
+        ds_parts.append(ds_product(0, QUARTERS[1], tag="q1_grouped"))
+        ds_parts.append(ds_product(0, HALVES[1], tag="q_raw1"))
+        for part, ds in zip((QUARTERS[0], QUARTERS[1], HALVES[1]), ds_parts):
+            ds_quantize(0, part, ds)
+        ds_parts = [ds_product(1, half) for half in HALVES]
         qm_first = mx_tiles("qm_first", PASSES * P)
-        for g in range(PASSES):
-            ds = sbuf("ds%d" % g, [P, N, PACK], BF16)
-            ds_mx.append(mx_tiles("ds%d" % g, N))
-            for half in HALVES:
-                nc.vector.tensor_tensor(
-                    ds[:, half, :].rearrange("p (c i) t -> p c t i", i=2),
-                    weights[g][:, :, half].rearrange("p t (c i) -> p c t i", i=2),
-                    gated[g][:, :, half].rearrange("p t (c i) -> p c t i", i=2),
-                    ALU.mult,
-                )
-            if g == PASSES - 1:
-                quantize_qm(0, qm_raw_first, 0, qm_first)
-            for half in HALVES:
-                quantize(ds_mx[g], half, ds[:, half, :].rearrange("p i t -> p (i t)"), E5M2)
+        quantize_qm(0, qm_raw_first, 0, qm_first)
+        for half, ds in zip(HALVES, ds_parts):
+            ds_quantize(1, half, ds)
 
         later_width = (D_TILES - 1) * PASSES * P
         qm_later = (
-            sbuf("qm_later_codes", [P, later_width], U32, tag="ds%d" % (PASSES - 1)),
+            sbuf("qm_later_codes", [P, later_width], U32, tag="ds1_%d" % HALVES[1].start),
             sbuf("qm_later_scales", [P, later_width], U8),
         )
         dk = []

@@ -51,7 +51,7 @@ def tile_attend_gat_lse_k_kernel(
 
         windows = [sbuf("window%d" % w, [P, T], F32) for w in range(WINDOWS)]
         for window in windows:
-            nc.gpsimd.memset(window[:], 0.0)
+            nc.vector.memset(window[:], 0.0)
 
         def load_rows(name, rows, pieces=1):
             raw = sbuf(name, [P, PACK, rows.shape[1]], F32)
@@ -88,16 +88,19 @@ def tile_attend_gat_lse_k_kernel(
         load_pool_scales(k_pool_scales, k_scales, range(2))
         v_pool_words = load_pool_words("v_pool_words", v_words)
         load_pool_scales(k_pool_scales, k_scales, range(2, 4))
+        do_raw[1] = load_rows("do_raw1", doT[0, :, queries(1)])
         q_raw[0] = load_rows("q_raw0", qT[0, :, queries(0)])
         k_pool_words = load_pool_words("k_pool_words", k_words)
-        do_raw[1] = load_rows("do_raw1", doT[0, :, queries(1)])
-        q_raw[1] = load_rows("q_raw1", qT[0, :, queries(1)])
+        q_raw[1] = [load_rows("q_raw1_%d" % half.start, qT[0, :, queries(1)][:, half]) for half in HALVES]
         qm_raw_first = [load_rows("qm_raw_first%d" % g, qm[0, queries(g), 0:P]) for g in range(PASSES)]
         qm_raw_later = [load_rows("qm_raw_later%d" % g, qm[0, queries(g), P:D]) for g in range(PASSES)]
 
-        def gather(name, window, dtype):
-            listed = sbuf(name, [P, N], dtype)
-            nc.vector.tensor_copy(listed[:], window[:].bitcast(dtype).indirect(offsets[:]))
+        def entries(part):
+            return offsets[:, part.start // 16 : part.stop // 16]
+
+        def gather(name, window, dtype, part=slice(0, N)):
+            listed = sbuf(name, [P, part.stop - part.start], dtype)
+            nc.vector.tensor_copy(listed[:], window[:].bitcast(dtype).indirect(entries(part)))
             return listed
 
         def mx_tiles(name, width, tag=None):
@@ -106,25 +109,25 @@ def tile_attend_gat_lse_k_kernel(
         def quantize(mx, columns, grouped, fmt):
             nc.vector.quantize_mx(out=mx[0][:, columns].bitcast(fmt), scales=mx[1][:, columns], in_=grouped)
 
-        def round_by_query(name, raw, shares, tag=None):
+        def round_by_query(name, shares, tag=None):
             grouped = sbuf(name + "_grouped", [P, PACK, P, PACK], BF16, tag=tag)
-            for copy, first, last in shares:
+            step = P // len(shares)
+            for index, (copy, raw) in enumerate(shares):
                 copy(
-                    grouped[:].rearrange("p t m j -> p m j t")[:, first:last],
-                    raw[:].rearrange("p j (m t) -> p m j t", t=PACK)[:, first:last],
+                    grouped[:].rearrange("p t m j -> p m j t")[:, index * step : (index + 1) * step],
+                    raw.rearrange("p j (m t) -> p m j t", t=PACK),
                 )
             return grouped
 
         def quantize_by_query(name, grouped, fmt, tag=None):
             mx = mx_tiles(name, K_PASS, tag)
-            for t in range(PACK):
-                quantize(mx, slice(t * P, (t + 1) * P), grouped[:, t, :, :].rearrange("p m j -> p (m j)"), fmt)
+            quantize(mx, slice(0, K_PASS), grouped[:].rearrange("p t m j -> p (t m j)"), fmt)
             return mx
 
         def multiply(acc, stationary, run, stationary_fmt, moving, moving_fmt, start, stop):
             columns = slice(run * P, (run + 1) * P)
             nc.tensor.matmul_mx(
-                out=acc[:],
+                out=acc,
                 lhsT=stationary[0][:, columns].bitcast(stationary_fmt),
                 lhsT_scale=stationary[1][:, columns],
                 rhs=moving[0][:].bitcast(moving_fmt),
@@ -134,34 +137,37 @@ def tile_attend_gat_lse_k_kernel(
             )
 
         gated = [sbuf("gated%d" % g, [P, PACK, N], F32) for g in range(PASSES)]
-        weights = [sbuf("weights%d" % g, [P, PACK, N], F32) for g in range(PASSES)]
-        ds_mx = [mx_tiles("ds%d" % g, N) for g in range(PASSES)]
+        weights = {}
+        ds_all = mx_tiles("ds", N // 2 + PASSES * N)
+        nc.gpsimd.memset(ds_all[0][:, 0 : N // 2].bitcast(I32), 0)
+        nc.gpsimd.memset(ds_all[1][:, 0 : N // 2].bitcast(I32), 0)
+        ds_mx = [[plane[:, N // 2 + g * N : N // 2 + (g + 1) * N] for plane in ds_all] for g in range(PASSES)]
+        ds_early = [[plane[:, g * N : (g + 1) * N] for plane in ds_all] for g in range(PASSES)]
 
         def gate(g, do_mx):
             for t in range(PACK):
                 dp = bank(PACK + t)
-                multiply(dp, do_mx, t, E5M2, values, E4M3, True, True)
+                multiply(dp[:], do_mx, t, E5M2, values, E4M3, True, True)
                 nc.scalar.activation(
                     gated[g][:, t, :], dp[:], ACT.Identity,
                     bias=neg_delta_rw[:, g, t : t + 1], scale=rw_q[:, g, t : t + 1],
                 )
 
-        def weigh(g, q_mx):
-            scores = []
-            for half in HALVES:
-                for t in range(PACK):
-                    if half.start == 0:
-                        scores.append(bank(t))
-                        multiply(scores[t], q_mx, t, E4M3, keys, E4M3, True, True)
-                    nc.scalar.activation(
-                        weights[g][:, t, half], scores[t][:, half], ACT.Exp, bias=neg_lse[:, g, t : t + 1]
-                    )
+        def weigh(g, q_mx, index, tag=None):
+            half = HALVES[index]
+            weights[g, half.start] = sbuf("weights%d_%d" % (g, index), [P, PACK, N // 2], F32, tag=tag)
+            for t in range(PACK):
+                scores = bank(t)[:, 0 : N // 2]
+                multiply(scores, q_mx, t, E4M3, (keys[0][index], keys[1][:, half]), E4M3, True, True)
+                nc.scalar.activation(
+                    weights[g, half.start][:, t, :], scores, ACT.Exp, bias=neg_lse[:, g, t : t + 1]
+                )
 
         def ds_product(g, part, tag=None):
             ds = sbuf("ds%d_%d" % (g, part.start), [P, part.stop - part.start, PACK], BF16, tag=tag)
             nc.vector.tensor_tensor(
                 ds[:].rearrange("p (c i) t -> p c t i", i=2),
-                weights[g][:, :, part].rearrange("p t (c i) -> p c t i", i=2),
+                weights[g, part.start // (N // 2) * (N // 2)][:, :, part.start % (N // 2) :][:, :, : part.stop - part.start].rearrange("p t (c i) -> p c t i", i=2),
                 gated[g][:, :, part].rearrange("p t (c i) -> p c t i", i=2),
                 ALU.mult,
             )
@@ -170,19 +176,22 @@ def tile_attend_gat_lse_k_kernel(
         def ds_quantize(g, part, ds):
             quantize(ds_mx[g], part, ds[:].rearrange("p i t -> p (i t)"), E5M2)
 
-        def quantize_qm(m, raw, raw_block, mx):
-            grouped = sbuf("qm_grouped%d" % m, [P, PASSES, P, PACK], BF16)
+        def round_qm(m, raw, raw_block, tag=None):
+            grouped = sbuf("qm_grouped%d" % m, [P, PASSES, P, PACK], BF16, tag=tag)
             for g in range(PASSES):
                 nc.scalar.copy(
                     grouped[:, g, :, :].rearrange("p (c i) t -> p c t i", i=4),
                     raw[g][:, :, raw_block * P : (raw_block + 1) * P].rearrange("p t (c i) -> p c t i", i=4),
                 )
-                run = PASSES * raw_block + g
-                quantize(mx, slice(run * P, (run + 1) * P), grouped[:, g, :, :].rearrange("p d t -> p (d t)"), E4M3)
+            return grouped
+
+        def quantize_qm(grouped, mx, first_run):
+            columns = slice(first_run * P, (first_run + PASSES) * P)
+            quantize(mx, columns, grouped[:].rearrange("p g d t -> p (g d t)"), E4M3)
 
         by_scalar, by_vector = nc.scalar.copy, nc.vector.tensor_copy
 
-        do_grouped = round_by_query("do0", do_raw[0], ((by_scalar, 0, P // 2), (by_vector, P // 2, P)))
+        do_grouped = round_by_query("do0", ((by_scalar, do_raw[0][:, :, HALVES[0]]), (by_vector, do_raw[0][:, :, HALVES[1]])))
         v_listed_scales = gather("v_scales", v_pool_scales, U8)
         do_mx = quantize_by_query("do0", do_grouped, E5M2, tag="v_pool_scales")
         values = (gather("v_codes", v_pool_words, U32), v_listed_scales)
@@ -192,45 +201,66 @@ def tile_attend_gat_lse_k_kernel(
         nc.scalar.mul(neg_lse[:], lse_q, -1.0)
         gate(0, do_mx)
         k_listed_scales = gather("k_scales", k_pool_scales, U8)
-        q_mx = quantize_by_query("q0", round_by_query("q0", q_raw[0], ((by_vector, 0, P),), tag="k_pool_scales"), E4M3)
-        keys = (gather("k_codes", k_pool_words, U32), k_listed_scales)
-        weigh(0, q_mx)
+        do_grouped = round_by_query("do1", ((by_vector, do_raw[1][:]),), tag="k_pool_scales")
+        gate(1, quantize_by_query("do1", do_grouped, E5M2))
 
-        do_mx = quantize_by_query("do1", round_by_query("do1", do_raw[1], ((by_vector, 0, P),)), E5M2)
-        gate(1, do_mx)
-        ds_parts = [ds_product(0, QUARTERS[0], tag="do1_grouped")]
-        q_mx = quantize_by_query("q1", round_by_query("q1", q_raw[1], ((by_vector, 0, P),)), E4M3)
-        weigh(1, q_mx)
-        ds_parts.append(ds_product(0, QUARTERS[1], tag="q1_grouped"))
-        ds_parts.append(ds_product(0, HALVES[1], tag="q_raw1"))
-        for part, ds in zip((QUARTERS[0], QUARTERS[1], HALVES[1]), ds_parts):
-            ds_quantize(0, part, ds)
-        ds_parts = [ds_product(1, half) for half in HALVES]
+        q_mx = quantize_by_query("q0", round_by_query("q0", ((by_vector, q_raw[0][:]),)), E4M3)
+        keys = ([gather("k_codes%d" % half.start, k_pool_words, U32, half) for half in HALVES], k_listed_scales)
+        weigh(0, q_mx, 0)
+        weigh(0, q_mx, 1)
+        q_grouped = round_by_query("q1", [(by_vector, raw[:]) for raw in q_raw[1]])
+        q_mx = quantize_by_query("q1", q_grouped, E4M3)
+        weigh(1, q_mx, 0)
+        qm_first_grouped = round_qm(0, qm_raw_first, 0)
+        weigh(1, q_mx, 1, tag="qm_raw_first1")
+        ds = [ds_product(0, half, tag=tag) for half, tag in zip(HALVES, ("q1_grouped", "q_raw1_%d" % HALVES[1].start))]
+        for half, product in zip(HALVES, ds):
+            ds_quantize(0, half, product)
         qm_first = mx_tiles("qm_first", PASSES * P)
-        quantize_qm(0, qm_raw_first, 0, qm_first)
-        for half, ds in zip(HALVES, ds_parts):
-            ds_quantize(1, half, ds)
+        quantize_qm(qm_first_grouped, qm_first, 0)
+
+        def key_gradient(bank_index, qm_mx, first_run, moving=ds_mx):
+            acc = bank(bank_index)
+            for g in range(PASSES):
+                multiply(acc[:], qm_mx, first_run + g, E4M3, moving[g], E5M2, g == 0, g == PASSES - 1)
+            return acc
+
+        def copy_out(name, acc, part):
+            dk = sbuf(name, [P, part.stop - part.start], F32)
+            nc.scalar.copy(dk[:], acc[:, part])
+            return dk
+
+        def scatter(window, part, dk):
+            nc.vector.tensor_copy(window[:].indirect(entries(part)), dk[:])
+
+        def store(m):
+            nc.sync.dma_start(out[m * P : (m + 1) * P, :], windows[m % WINDOWS][:])
+
+        parts = (HALVES[0], QUARTERS[2], QUARTERS[3])
+        ds = [ds_product(1, part) for part in parts[:2]]
+        ds_quantize(1, parts[0], ds[0])
+        early_acc = key_gradient(PACK, qm_first, 0, ds_early)
+        ds.append(ds_product(1, parts[2]))
+        ds_quantize(1, parts[1], ds[1])
+        ds_quantize(1, parts[2], ds[2])
+        acc = key_gradient(PACK + 1, qm_first, 0)
 
         later_width = (D_TILES - 1) * PASSES * P
         qm_later = (
-            sbuf("qm_later_codes", [P, later_width], U32, tag="ds1_%d" % HALVES[1].start),
+            sbuf("qm_later_codes", [P, later_width], U32, tag="ds1_%d" % parts[1].start),
             sbuf("qm_later_scales", [P, later_width], U8),
         )
-        dk = []
-        for m in range(D_TILES):
-            qm_mx, first_run = (qm_first, 0) if m == 0 else (qm_later, (m - 1) * PASSES)
-            if m > 0:
-                quantize_qm(m, qm_raw_later, m - 1, qm_later)
-            acc = bank(m)
-            for g in range(PASSES):
-                multiply(acc, qm_mx, first_run + g, E4M3, ds_mx[g], E5M2, g == 0, g == PASSES - 1)
-            dk.append(sbuf("dk%d" % m, [P, N], F32))
-            for part in HALVES if m == 0 else (slice(0, N),):
-                nc.scalar.copy(dk[m][:, part], acc[:, part])
 
+        def prepare(m):
+            quantize_qm(round_qm(m, qm_raw_later, m - 1, tag=(None, "neg_lse", "qm_raw_first1", "gated1")[m]), qm_later, (m - 1) * PASSES)
+            return key_gradient(m, qm_later, (m - 1) * PASSES)
+
+        accs = [acc, prepare(1)]
+        early_dk = copy_out("early_dk", early_acc, HALVES[1])
+        scatter(windows[0], HALVES[0], early_dk)
         for m in range(D_TILES):
-            window = windows[m % WINDOWS]
-            for part in HALVES if m == 0 else (slice(0, N),):
-                entries = offsets[:, part.start // 16 : part.stop // 16]
-                nc.vector.tensor_copy(window[:].indirect(entries), dk[m][:, part])
-            nc.sync.dma_start(out[m * P : (m + 1) * P, :], window[:])
+            if m + 2 < D_TILES:
+                accs.append(prepare(m + 2))
+            part = HALVES[1] if m == 0 else slice(0, N)
+            scatter(windows[m % WINDOWS], part, copy_out("dk%d" % m, accs[m], part))
+            store(m)

@@ -23,6 +23,8 @@ PASSES = R // K_PASS
 D_TILES = D // P
 HALVES = (slice(0, N // 2), slice(N // 2, N))
 QUARTERS = tuple(slice(c * N // 4, (c + 1) * N // 4) for c in range(4))
+PLACES = {"do_raw1": 0, "k_scales": 0, "gated0": N}
+K_PLANE = 4
 WINDOWS = 3
 
 
@@ -32,9 +34,12 @@ def tile_attend_gat_lse_k_kernel(
     nc = tc.nc
     with ExitStack() as ctx:
         keep = ctx.enter_context(tc.tile_pool(name="keep", bufs=1))
+        placed = ctx.enter_context(tc.tile_pool(name="placed", bufs=1))
         psum = ctx.enter_context(tc.psum_pool(name="psum", bufs=1))
 
         def sbuf(name, shape, dtype, tag=None):
+            if name in PLACES:
+                return placed.tile(shape, dtype, name=name, align_bytes=64, offset=PLACES[name])
             return keep.tile(shape, dtype, name=name, tag=tag or name, align_bytes=64)
 
         def bank(index):
@@ -70,9 +75,9 @@ def tile_attend_gat_lse_k_kernel(
             nc.sync.dma_start(pool_words[:], words[0].rearrange("p t j -> p (t j)").bitcast(I32))
             return pool_words
 
-        def load_pool_scales(pool_scales, scales, rows):
+        def load_pool_scales(pool_scales, scales, rows, first=0):
             for row in rows:
-                nc.sync.dma_start(pool_scales[row:P:32, :], scales[0, row:16:4, :].bitcast(I32))
+                nc.sync.dma_start(pool_scales[first + row : P : 32, :], scales[0, row:16:4, :].bitcast(I32))
 
         def queries(g):
             return slice(g * K_PASS, (g + 1) * K_PASS)
@@ -85,9 +90,9 @@ def tile_attend_gat_lse_k_kernel(
         lse_q = load_per_query("lse_q", lse)
         do_raw[0] = load_rows("do_raw0", doT[0, :, queries(0)], pieces=2)
         load_pool_scales(v_pool_scales, v_scales, range(4))
-        load_pool_scales(k_pool_scales, k_scales, range(2))
+        load_pool_scales(k_pool_scales, k_scales, range(2), K_PLANE)
         v_pool_words = load_pool_words("v_pool_words", v_words)
-        load_pool_scales(k_pool_scales, k_scales, range(2, 4))
+        load_pool_scales(k_pool_scales, k_scales, range(2, 4), K_PLANE)
         do_raw[1] = load_rows("do_raw1", doT[0, :, queries(1)])
         q_raw[0] = load_rows("q_raw0", qT[0, :, queries(0)])
         k_pool_words = load_pool_words("k_pool_words", k_words)
@@ -158,7 +163,7 @@ def tile_attend_gat_lse_k_kernel(
             weights[g, half.start] = sbuf("weights%d_%d" % (g, index), [P, PACK, N // 2], F32, tag=tag)
             for t in range(PACK):
                 scores = bank(t)[:, 0 : N // 2]
-                multiply(scores, q_mx, t, E4M3, (keys[0][index], keys[1][:, half]), E4M3, True, True)
+                multiply(scores, q_mx, t, E4M3, (keys[0][index], keys[1][K_PLANE:, half]), E4M3, True, True)
                 nc.scalar.activation(
                     weights[g, half.start][:, t, :], scores, ACT.Exp, bias=neg_lse[:, g, t : t + 1]
                 )
@@ -191,7 +196,7 @@ def tile_attend_gat_lse_k_kernel(
 
         by_scalar, by_vector = nc.scalar.copy, nc.vector.tensor_copy
 
-        do_grouped = round_by_query("do0", ((by_scalar, do_raw[0][:, :, HALVES[0]]), (by_vector, do_raw[0][:, :, HALVES[1]])))
+        do_grouped = round_by_query("do0", ((by_scalar, do_raw[0][:]),))
         v_listed_scales = gather("v_scales", v_pool_scales, U8)
         do_mx = quantize_by_query("do0", do_grouped, E5M2, tag="v_pool_scales")
         values = (gather("v_codes", v_pool_words, U32), v_listed_scales)
@@ -199,12 +204,12 @@ def tile_attend_gat_lse_k_kernel(
         nc.vector.scalar_tensor_tensor(neg_delta_rw[:], delta_q, -1.0, rw_q, ALU.mult, ALU.mult)
         neg_lse = sbuf("neg_lse", [P, PASSES, PACK], F32)
         nc.scalar.mul(neg_lse[:], lse_q, -1.0)
-        gate(0, do_mx)
         k_listed_scales = gather("k_scales", k_pool_scales, U8)
-        do_grouped = round_by_query("do1", ((by_vector, do_raw[1][:]),), tag="k_pool_scales")
+        do_grouped = round_by_query("do1", ((by_scalar, do_raw[1][:, :, HALVES[0]]), (by_vector, do_raw[1][:, :, HALVES[1]])))
+        gate(0, do_mx)
         gate(1, quantize_by_query("do1", do_grouped, E5M2))
 
-        q_mx = quantize_by_query("q0", round_by_query("q0", ((by_vector, q_raw[0][:]),)), E4M3)
+        q_mx = quantize_by_query("q0", round_by_query("q0", ((by_vector, q_raw[0][:]),), tag="k_pool_scales"), E4M3)
         keys = ([gather("k_codes%d" % half.start, k_pool_words, U32, half) for half in HALVES], k_listed_scales)
         weigh(0, q_mx, 0)
         weigh(0, q_mx, 1)

@@ -21,10 +21,11 @@ PACK = 4
 K_PASS = P * PACK
 PASSES = R // K_PASS
 D_TILES = D // P
-HALVES = (slice(0, N // 2), slice(N // 2, N))
+HALF = N // 2
+HALVES = (slice(0, HALF), slice(HALF, N))
 QUARTERS = tuple(slice(c * N // 4, (c + 1) * N // 4) for c in range(4))
-PLACES = {"do_raw1": 0, "k_scales": 0, "gated0": N}
 K_PLANE = 4
+PLACES = {"q1_grouped": 0, "ds0_128": 0, "ds0_256": 1024}
 WINDOWS = 3
 
 
@@ -50,19 +51,16 @@ def tile_attend_gat_lse_k_kernel(
         k_pool_scales = sbuf("k_pool_scales", [P, T // 4], I32)
         nc.vector.memset(k_pool_scales[:], 0)
 
-        warm = sbuf("warm", [P, 2], F32)
-        nc.gpsimd.memset(warm[:, 0:1], 0.0)
-        nc.scalar.activation(warm[:, 1:2], warm[:, 0:1], ACT.Exp)
-
         windows = [sbuf("window%d" % w, [P, T], F32) for w in range(WINDOWS)]
         for window in windows:
             nc.vector.memset(window[:], 0.0)
 
         def load_rows(name, rows, pieces=1):
             raw = sbuf(name, [P, PACK, rows.shape[1]], F32)
+            by_partition = rows.rearrange("(p j) c -> p j c", j=PACK)
             step = PACK // pieces
             for j in range(0, PACK, step):
-                nc.sync.dma_start(raw[:, j : j + step, :], rows.rearrange("(p j) c -> p j c", j=PACK)[:, j : j + step, :])
+                nc.sync.dma_start(raw[:, j : j + step, :], by_partition[:, j : j + step, :])
             return raw
 
         def load_per_query(name, values):
@@ -114,15 +112,14 @@ def tile_attend_gat_lse_k_kernel(
         def quantize(mx, columns, grouped, fmt):
             nc.vector.quantize_mx(out=mx[0][:, columns].bitcast(fmt), scales=mx[1][:, columns], in_=grouped)
 
-        def round_by_query(name, shares, tag=None):
-            grouped = sbuf(name + "_grouped", [P, PACK, P, PACK], BF16, tag=tag)
-            step = P // len(shares)
-            for index, (copy, raw) in enumerate(shares):
-                copy(
-                    grouped[:].rearrange("p t m j -> p m j t")[:, index * step : (index + 1) * step],
-                    raw.rearrange("p j (m t) -> p m j t", t=PACK),
-                )
-            return grouped
+        def round_by_query(grouped, copy, raw, m_range=slice(0, P)):
+            copy(
+                grouped[:].rearrange("p t m j -> p m j t")[:, m_range],
+                raw[:].rearrange("p j (m t) -> p m j t", t=PACK),
+            )
+
+        def grouped_tile(name, tag=None):
+            return sbuf(name + "_grouped", [P, PACK, P, PACK], BF16, tag=tag)
 
         def quantize_by_query(name, grouped, fmt, tag=None):
             mx = mx_tiles(name, K_PASS, tag)
@@ -143,11 +140,11 @@ def tile_attend_gat_lse_k_kernel(
 
         gated = [sbuf("gated%d" % g, [P, PACK, N], F32) for g in range(PASSES)]
         weights = {}
-        ds_all = mx_tiles("ds", N // 2 + PASSES * N)
-        nc.gpsimd.memset(ds_all[0][:, 0 : N // 2].bitcast(I32), 0)
-        nc.gpsimd.memset(ds_all[1][:, 0 : N // 2].bitcast(I32), 0)
-        ds_mx = [[plane[:, N // 2 + g * N : N // 2 + (g + 1) * N] for plane in ds_all] for g in range(PASSES)]
-        ds_early = [[plane[:, g * N : (g + 1) * N] for plane in ds_all] for g in range(PASSES)]
+        ds_all = mx_tiles("ds", HALF + PASSES * N)
+        nc.gpsimd.memset(ds_all[0][:, 0:HALF].bitcast(I32), 0)
+        nc.gpsimd.memset(ds_all[1][:, 0:HALF].bitcast(I32), 0)
+        ds_mx = [[tile[:, HALF + g * N : HALF + (g + 1) * N] for tile in ds_all] for g in range(PASSES)]
+        ds_early = [[tile[:, g * N : (g + 1) * N] for tile in ds_all] for g in range(PASSES)]
 
         def gate(g, do_mx):
             for t in range(PACK):
@@ -158,21 +155,27 @@ def tile_attend_gat_lse_k_kernel(
                     bias=neg_delta_rw[:, g, t : t + 1], scale=rw_q[:, g, t : t + 1],
                 )
 
-        def weigh(g, q_mx, index, tag=None):
-            half = HALVES[index]
-            weights[g, half.start] = sbuf("weights%d_%d" % (g, index), [P, PACK, N // 2], F32, tag=tag)
-            for t in range(PACK):
-                scores = bank(t)[:, 0 : N // 2]
-                multiply(scores, q_mx, t, E4M3, (keys[0][index], keys[1][K_PLANE:, half]), E4M3, True, True)
-                nc.scalar.activation(
-                    weights[g, half.start][:, t, :], scores, ACT.Exp, bias=neg_lse[:, g, t : t + 1]
-                )
+        def weigh(g, q_mx, index, tag=None, rounds=1):
+            weights[g, index] = sbuf("weights%d_%d" % (g, index), [P, PACK, HALF], F32, tag=tag)
+            moving = (k_listed_codes[index], k_listed_scales[K_PLANE:, HALVES[index]])
+            scores = [bank(t) for t in range(PACK)]
+            width = HALF // rounds
+            for first in range(0, HALF, width):
+                for t in range(PACK):
+                    if first == 0:
+                        multiply(scores[t][:, 0:HALF], q_mx, t, E4M3, moving, E4M3, True, True)
+                    nc.scalar.activation(
+                        weights[g, index][:, t, first : first + width], scores[t][:, first : first + width],
+                        ACT.Exp, bias=neg_lse[:, g, t : t + 1],
+                    )
 
         def ds_product(g, part, tag=None):
-            ds = sbuf("ds%d_%d" % (g, part.start), [P, part.stop - part.start, PACK], BF16, tag=tag)
+            width = part.stop - part.start
+            index, first = divmod(part.start, HALF)
+            ds = sbuf("ds%d_%d" % (g, part.start), [P, width, PACK], BF16, tag=tag)
             nc.vector.tensor_tensor(
                 ds[:].rearrange("p (c i) t -> p c t i", i=2),
-                weights[g, part.start // (N // 2) * (N // 2)][:, :, part.start % (N // 2) :][:, :, : part.stop - part.start].rearrange("p t (c i) -> p c t i", i=2),
+                weights[g, index][:, :, first : first + width].rearrange("p t (c i) -> p c t i", i=2),
                 gated[g][:, :, part].rearrange("p t (c i) -> p c t i", i=2),
                 ALU.mult,
             )
@@ -196,7 +199,8 @@ def tile_attend_gat_lse_k_kernel(
 
         by_scalar, by_vector = nc.scalar.copy, nc.vector.tensor_copy
 
-        do_grouped = round_by_query("do0", ((by_scalar, do_raw[0][:]),))
+        do_grouped = grouped_tile("do0")
+        round_by_query(do_grouped, by_scalar, do_raw[0])
         v_listed_scales = gather("v_scales", v_pool_scales, U8)
         do_mx = quantize_by_query("do0", do_grouped, E5M2, tag="v_pool_scales")
         values = (gather("v_codes", v_pool_words, U32), v_listed_scales)
@@ -205,22 +209,31 @@ def tile_attend_gat_lse_k_kernel(
         neg_lse = sbuf("neg_lse", [P, PASSES, PACK], F32)
         nc.scalar.mul(neg_lse[:], lse_q, -1.0)
         k_listed_scales = gather("k_scales", k_pool_scales, U8)
-        do_grouped = round_by_query("do1", ((by_scalar, do_raw[1][:, :, HALVES[0]]), (by_vector, do_raw[1][:, :, HALVES[1]])))
         gate(0, do_mx)
+        do_grouped = grouped_tile("do1", tag="k_pool_scales")
+        round_by_query(do_grouped, by_vector, do_raw[1])
         gate(1, quantize_by_query("do1", do_grouped, E5M2))
 
-        q_mx = quantize_by_query("q0", round_by_query("q0", ((by_vector, q_raw[0][:]),), tag="k_pool_scales"), E4M3)
-        keys = ([gather("k_codes%d" % half.start, k_pool_words, U32, half) for half in HALVES], k_listed_scales)
-        weigh(0, q_mx, 0)
+        q_grouped = grouped_tile("q0")
+        round_by_query(q_grouped, by_vector, q_raw[0])
+        q_mx = quantize_by_query("q0", q_grouped, E4M3)
+        k_listed_codes = [gather("k_codes%d" % half.start, k_pool_words, U32, half) for half in HALVES]
+        weigh(0, q_mx, 0, rounds=2)
         weigh(0, q_mx, 1)
-        q_grouped = round_by_query("q1", [(by_vector, raw[:]) for raw in q_raw[1]])
+
+        q_grouped = grouped_tile("q1")
+        round_by_query(q_grouped, by_vector, q_raw[1][0], slice(0, P // 2))
+        first_quarter = ds_product(0, QUARTERS[0], tag="q_raw1_0")
+        round_by_query(q_grouped, by_vector, q_raw[1][1], slice(P // 2, P))
+        ds_quantize(0, QUARTERS[0], first_quarter)
         q_mx = quantize_by_query("q1", q_grouped, E4M3)
         weigh(1, q_mx, 0)
         qm_first_grouped = round_qm(0, qm_raw_first, 0)
         weigh(1, q_mx, 1, tag="qm_raw_first1")
-        ds = [ds_product(0, half, tag=tag) for half, tag in zip(HALVES, ("q1_grouped", "q_raw1_%d" % HALVES[1].start))]
-        for half, product in zip(HALVES, ds):
-            ds_quantize(0, half, product)
+        second_quarter = ds_product(0, QUARTERS[1])
+        second_half = ds_product(0, HALVES[1])
+        ds_quantize(0, QUARTERS[1], second_quarter)
+        ds_quantize(0, HALVES[1], second_half)
         qm_first = mx_tiles("qm_first", PASSES * P)
         quantize_qm(qm_first_grouped, qm_first, 0)
 
@@ -238,34 +251,33 @@ def tile_attend_gat_lse_k_kernel(
         def scatter(window, part, dk):
             nc.vector.tensor_copy(window[:].indirect(entries(part)), dk[:])
 
-        def store(m):
-            nc.sync.dma_start(out[m * P : (m + 1) * P, :], windows[m % WINDOWS][:])
-
-        parts = (HALVES[0], QUARTERS[2], QUARTERS[3])
-        ds = [ds_product(1, part) for part in parts[:2]]
-        ds_quantize(1, parts[0], ds[0])
+        first_half = ds_product(1, HALVES[0])
+        third_quarter = ds_product(1, QUARTERS[2])
+        ds_quantize(1, HALVES[0], first_half)
         early_acc = key_gradient(PACK, qm_first, 0, ds_early)
-        ds.append(ds_product(1, parts[2]))
-        ds_quantize(1, parts[1], ds[1])
-        ds_quantize(1, parts[2], ds[2])
-        acc = key_gradient(PACK + 1, qm_first, 0)
+        last_quarter = ds_product(1, QUARTERS[3])
+        ds_quantize(1, QUARTERS[2], third_quarter)
+        ds_quantize(1, QUARTERS[3], last_quarter)
+        accs = [key_gradient(PACK + 1, qm_first, 0)]
 
         later_width = (D_TILES - 1) * PASSES * P
         qm_later = (
-            sbuf("qm_later_codes", [P, later_width], U32, tag="ds1_%d" % parts[1].start),
+            sbuf("qm_later_codes", [P, later_width], U32, tag="ds1_%d" % QUARTERS[2].start),
             sbuf("qm_later_scales", [P, later_width], U8),
         )
+        freed_tags = {1: "neg_lse", 2: "qm_raw_first1", 3: "gated1"}
 
-        def prepare(m):
-            quantize_qm(round_qm(m, qm_raw_later, m - 1, tag=(None, "neg_lse", "qm_raw_first1", "gated1")[m]), qm_later, (m - 1) * PASSES)
-            return key_gradient(m, qm_later, (m - 1) * PASSES)
+        def later_gradient(m):
+            first_run = (m - 1) * PASSES
+            quantize_qm(round_qm(m, qm_raw_later, m - 1, tag=freed_tags[m]), qm_later, first_run)
+            return key_gradient(m, qm_later, first_run)
 
-        accs = [acc, prepare(1)]
-        early_dk = copy_out("early_dk", early_acc, HALVES[1])
-        scatter(windows[0], HALVES[0], early_dk)
+        accs.append(later_gradient(1))
+        scatter(windows[0], HALVES[0], copy_out("early_dk", early_acc, HALVES[1]))
         for m in range(D_TILES):
             if m + 2 < D_TILES:
-                accs.append(prepare(m + 2))
+                accs.append(later_gradient(m + 2))
+            window = windows[m % WINDOWS]
             part = HALVES[1] if m == 0 else slice(0, N)
-            scatter(windows[m % WINDOWS], part, copy_out("dk%d" % m, accs[m], part))
-            store(m)
+            scatter(window, part, copy_out("dk%d" % m, accs[m], part))
+            nc.sync.dma_start(out[m * P : (m + 1) * P, :], window[:])

@@ -25,7 +25,7 @@ HALF = N // 2
 HALVES = (slice(0, HALF), slice(HALF, N))
 QUARTERS = tuple(slice(c * N // 4, (c + 1) * N // 4) for c in range(4))
 K_PLANE = 4
-PLACES = {"q1_grouped": 0, "ds0_128": 0, "ds0_256": 1024}
+PLACES = {"q1_grouped": 0, "ds0_128": 0, "ds0_256": 1024, "qm_grouped2": 4096, "qm_grouped3": 6144, "dk0_1": 5632}
 WINDOWS = 3
 
 
@@ -140,11 +140,7 @@ def tile_attend_gat_lse_k_kernel(
 
         gated = [sbuf("gated%d" % g, [P, PACK, N], F32) for g in range(PASSES)]
         weights = {}
-        ds_all = mx_tiles("ds", HALF + PASSES * N)
-        nc.gpsimd.memset(ds_all[0][:, 0:HALF].bitcast(I32), 0)
-        nc.gpsimd.memset(ds_all[1][:, 0:HALF].bitcast(I32), 0)
-        ds_mx = [[tile[:, HALF + g * N : HALF + (g + 1) * N] for tile in ds_all] for g in range(PASSES)]
-        ds_early = [[tile[:, g * N : (g + 1) * N] for tile in ds_all] for g in range(PASSES)]
+        ds_mx = [mx_tiles("ds%d" % g, N) for g in range(PASSES)]
 
         def gate(g, do_mx):
             for t in range(PACK):
@@ -184,10 +180,10 @@ def tile_attend_gat_lse_k_kernel(
         def ds_quantize(g, part, ds):
             quantize(ds_mx[g], part, ds[:].rearrange("p i t -> p (i t)"), E5M2)
 
-        def round_qm(m, raw, raw_block, tag=None):
+        def round_qm(m, raw, raw_block, copy, tag=None):
             grouped = sbuf("qm_grouped%d" % m, [P, PASSES, P, PACK], BF16, tag=tag)
             for g in range(PASSES):
-                nc.scalar.copy(
+                copy(
                     grouped[:, g, :, :].rearrange("p (c i) t -> p c t i", i=4),
                     raw[g][:, :, raw_block * P : (raw_block + 1) * P].rearrange("p t (c i) -> p c t i", i=4),
                 )
@@ -228,56 +224,67 @@ def tile_attend_gat_lse_k_kernel(
         ds_quantize(0, QUARTERS[0], first_quarter)
         q_mx = quantize_by_query("q1", q_grouped, E4M3)
         weigh(1, q_mx, 0)
-        qm_first_grouped = round_qm(0, qm_raw_first, 0)
+        qm_first_grouped = round_qm(0, qm_raw_first, 0, by_scalar)
         weigh(1, q_mx, 1, tag="qm_raw_first1")
         second_quarter = ds_product(0, QUARTERS[1])
         second_half = ds_product(0, HALVES[1])
         ds_quantize(0, QUARTERS[1], second_quarter)
+        first_half = ds_product(1, HALVES[0])
         ds_quantize(0, HALVES[1], second_half)
         qm_first = mx_tiles("qm_first", PASSES * P)
         quantize_qm(qm_first_grouped, qm_first, 0)
+        ds_quantize(1, HALVES[0], first_half)
 
-        def key_gradient(bank_index, qm_mx, first_run, moving=ds_mx):
-            acc = bank(bank_index)
+        def key_gradient(m, index, qm_mx, first_run):
+            acc = bank((PACK + 2 * m + index) % (2 * PACK))[:, 0:HALF]
             for g in range(PASSES):
-                multiply(acc[:], qm_mx, first_run + g, E4M3, moving[g], E5M2, g == 0, g == PASSES - 1)
+                moving = [tile[:, HALVES[index]] for tile in ds_mx[g]]
+                multiply(acc, qm_mx, first_run + g, E4M3, moving, E5M2, g == 0, g == PASSES - 1)
             return acc
 
-        def copy_out(name, acc, part):
-            dk = sbuf(name, [P, part.stop - part.start], F32)
-            nc.scalar.copy(dk[:], acc[:, part])
+        def copy_out(m, index, acc, copy):
+            dk = sbuf("dk%d_%d" % (m, index), [P, HALF], F32)
+            copy(dk[:], acc)
             return dk
 
-        def scatter(window, part, dk):
-            nc.vector.tensor_copy(window[:].indirect(entries(part)), dk[:])
+        def scatter_by_vector(m, index, dk):
+            nc.vector.tensor_copy(windows[m % WINDOWS][:].indirect(entries(HALVES[index])), dk[:])
 
-        first_half = ds_product(1, HALVES[0])
+        def scatter_by_scalar(m, index, dk):
+            nc.scalar.activation(windows[m % WINDOWS][:].indirect(entries(HALVES[index])), dk[:], ACT.Copy)
+
+        def store(m):
+            nc.sync.dma_start(out[m * P : (m + 1) * P, :], windows[m % WINDOWS][:])
+
+        first_dk = copy_out(0, 0, key_gradient(0, 0, qm_first, 0), by_scalar)
+        scatter_by_scalar(0, 0, first_dk)
         third_quarter = ds_product(1, QUARTERS[2])
-        ds_quantize(1, HALVES[0], first_half)
-        early_acc = key_gradient(PACK, qm_first, 0, ds_early)
         last_quarter = ds_product(1, QUARTERS[3])
         ds_quantize(1, QUARTERS[2], third_quarter)
         ds_quantize(1, QUARTERS[3], last_quarter)
-        accs = [key_gradient(PACK + 1, qm_first, 0)]
+        last_dk = copy_out(0, 1, key_gradient(0, 1, qm_first, 0), by_scalar)
 
-        later_width = (D_TILES - 1) * PASSES * P
-        qm_later = (
-            sbuf("qm_later_codes", [P, later_width], U32, tag="ds1_%d" % QUARTERS[2].start),
-            sbuf("qm_later_scales", [P, later_width], U8),
-        )
-        freed_tags = {1: "neg_lse", 2: "qm_raw_first1", 3: "gated1"}
+        qm_later = mx_tiles("qm_later", (D_TILES - 1) * PASSES * P)
 
-        def later_gradient(m):
-            first_run = (m - 1) * PASSES
-            quantize_qm(round_qm(m, qm_raw_later, m - 1, tag=freed_tags[m]), qm_later, first_run)
-            return key_gradient(m, qm_later, first_run)
+        def quantize_later(m, grouped):
+            for g in range(PASSES):
+                run = (m - 1) * PASSES + g
+                quantize(qm_later, slice(run * P, (run + 1) * P), grouped[:, g].rearrange("p d t -> p (d t)"), E4M3)
 
-        accs.append(later_gradient(1))
-        scatter(windows[0], HALVES[0], copy_out("early_dk", early_acc, HALVES[1]))
-        for m in range(D_TILES):
-            if m + 2 < D_TILES:
-                accs.append(later_gradient(m + 2))
-            window = windows[m % WINDOWS]
-            part = HALVES[1] if m == 0 else slice(0, N)
-            scatter(window, part, copy_out("dk%d" % m, accs[m], part))
-            nc.sync.dma_start(out[m * P : (m + 1) * P, :], window[:])
+        def place_block(m, copy, scatter):
+            for index in range(len(HALVES)):
+                scatter(m, index, copy_out(m, index, key_gradient(m, index, qm_later, (m - 1) * PASSES), copy))
+            store(m)
+
+        quantize_later(1, round_qm(1, qm_raw_later, 0, by_vector, tag="gated1"))
+        scatter_by_vector(0, 1, last_dk)
+        store(0)
+        place_block(1, by_scalar, scatter_by_scalar)
+        quantize_later(2, round_qm(2, qm_raw_later, 1, by_vector))
+        last_grouped = round_qm(3, qm_raw_later, 2, by_vector)
+        dk = copy_out(2, 0, key_gradient(2, 0, qm_later, PASSES), by_vector)
+        quantize_later(3, last_grouped)
+        scatter_by_vector(2, 0, dk)
+        scatter_by_vector(2, 1, copy_out(2, 1, key_gradient(2, 1, qm_later, PASSES), by_scalar))
+        store(2)
+        place_block(3, by_scalar, scatter_by_scalar)

@@ -25,8 +25,9 @@ HALF = N // 2
 HALVES = (slice(0, HALF), slice(HALF, N))
 QUARTERS = tuple(slice(c * N // 4, (c + 1) * N // 4) for c in range(4))
 K_PLANE = 4
-PLACES = {"q1_grouped": 0, "ds0_128": 0, "ds0_256": 1024, "qm_grouped2": 4096, "qm_grouped3": 6144, "dk0_1": 5632}
-WINDOWS = 3
+PLACES = {"q1_grouped": 0, "ds0_128": 0, "ds0_256": 1024, "qm_grouped3": 4096, "dk0_1": 4096,
+          "gated1": 8192, "qm_grouped1": 8192, "qm_grouped2": 10240}
+WINDOWS = 4
 
 
 def tile_attend_gat_lse_k_kernel(
@@ -266,25 +267,35 @@ def tile_attend_gat_lse_k_kernel(
 
         qm_later = mx_tiles("qm_later", (D_TILES - 1) * PASSES * P)
 
-        def quantize_later(m, grouped):
-            for g in range(PASSES):
-                run = (m - 1) * PASSES + g
-                quantize(qm_later, slice(run * P, (run + 1) * P), grouped[:, g].rearrange("p d t -> p (d t)"), E4M3)
+        def round_later(m):
+            return round_qm(m, qm_raw_later, m - 1, by_vector)
 
-        def place_block(m, copy, scatter):
+        def quantize_later(m, g, grouped):
+            run = (m - 1) * PASSES + g
+            quantize(qm_later, slice(run * P, (run + 1) * P), grouped[:, g].rearrange("p d t -> p (d t)"), E4M3)
+
+        def later_dk(m, index, copy):
+            return copy_out(m, index, key_gradient(m, index, qm_later, (m - 1) * PASSES), copy)
+
+        def place_block(m):
             for index in range(len(HALVES)):
-                scatter(m, index, copy_out(m, index, key_gradient(m, index, qm_later, (m - 1) * PASSES), copy))
+                scatter_by_scalar(m, index, later_dk(m, index, by_scalar))
             store(m)
 
-        quantize_later(1, round_qm(1, qm_raw_later, 0, by_vector, tag="gated1"))
+        second_grouped = round_later(1)
+        quantize_later(1, 0, second_grouped)
+        third_grouped = round_later(2)
+        quantize_later(1, 1, second_grouped)
+        for g in range(PASSES):
+            quantize_later(2, g, third_grouped)
         scatter_by_vector(0, 1, last_dk)
         store(0)
-        place_block(1, by_scalar, scatter_by_scalar)
-        quantize_later(2, round_qm(2, qm_raw_later, 1, by_vector))
-        last_grouped = round_qm(3, qm_raw_later, 2, by_vector)
-        dk = copy_out(2, 0, key_gradient(2, 0, qm_later, PASSES), by_vector)
-        quantize_later(3, last_grouped)
+        place_block(1)
+        last_grouped = round_later(3)
+        dk = later_dk(2, 0, by_vector)
+        for g in range(PASSES):
+            quantize_later(3, g, last_grouped)
         scatter_by_vector(2, 0, dk)
-        scatter_by_vector(2, 1, copy_out(2, 1, key_gradient(2, 1, qm_later, PASSES), by_scalar))
+        scatter_by_vector(2, 1, later_dk(2, 1, by_scalar))
         store(2)
-        place_block(3, by_scalar, scatter_by_scalar)
+        place_block(3)

@@ -24,9 +24,13 @@ D_TILES = D // P
 HALF = N // 2
 HALVES = (slice(0, HALF), slice(HALF, N))
 QUARTERS = tuple(slice(c * N // 4, (c + 1) * N // 4) for c in range(4))
+RUN_PAIRS = (slice(0, 2), slice(2, PACK))
 K_PLANE = 4
-PLACES = {"q1_grouped": 0, "ds0_128": 0, "ds0_256": 1024, "qm_grouped3": 4096, "dk0_1": 4096,
-          "gated1": 8192, "qm_grouped1": 8192, "qm_grouped2": 10240}
+PLACES = {
+    "q1_grouped": 0, "ds0_128": 0, "ds0_256": 1024,
+    "dk0_256": 4096, "qm3_1_codes": 4096,
+    "gated1": 8192, "qm_grouped2_0": 8192, "qm_grouped2_1": 9216, "qm_grouped3_0": 10240, "dk1_256": 10240, "qm_grouped3_1": 11264,
+}
 WINDOWS = 4
 
 
@@ -96,8 +100,8 @@ def tile_attend_gat_lse_k_kernel(
         q_raw[0] = load_rows("q_raw0", qT[0, :, queries(0)])
         k_pool_words = load_pool_words("k_pool_words", k_words)
         q_raw[1] = [load_rows("q_raw1_%d" % half.start, qT[0, :, queries(1)][:, half]) for half in HALVES]
-        qm_raw_first = [load_rows("qm_raw_first%d" % g, qm[0, queries(g), 0:P]) for g in range(PASSES)]
-        qm_raw_later = [load_rows("qm_raw_later%d" % g, qm[0, queries(g), P:D]) for g in range(PASSES)]
+        qm_raw_first = [load_rows("qm_raw_first%d" % g, qm[0, queries(g), 0 : D // 2]) for g in range(PASSES)]
+        qm_raw_later = [load_rows("qm_raw_later%d" % g, qm[0, queries(g), D // 2 : D]) for g in range(PASSES)]
 
         def entries(part):
             return offsets[:, part.start // 16 : part.stop // 16]
@@ -113,11 +117,24 @@ def tile_attend_gat_lse_k_kernel(
         def quantize(mx, columns, grouped, fmt):
             nc.vector.quantize_mx(out=mx[0][:, columns].bitcast(fmt), scales=mx[1][:, columns], in_=grouped)
 
-        def round_by_query(grouped, copy, raw, m_range=slice(0, P)):
+        def round_by_query(grouped, copy, raw, m_range=slice(0, P), runs=slice(0, PACK)):
             copy(
-                grouped[:].rearrange("p t m j -> p m j t")[:, m_range],
-                raw[:].rearrange("p j (m t) -> p m j t", t=PACK),
+                grouped[:].rearrange("p t m j -> p m j t")[:, m_range, :, runs],
+                raw[:].rearrange("p j (m t) -> p m j t", t=PACK)[:, :, :, runs],
             )
+
+        def quantize_runs(mx, grouped, runs, fmt):
+            columns = slice(runs.start * P, runs.stop * P)
+            quantize(mx, columns, grouped[:, runs].rearrange("p t m j -> p (t m j)"), fmt)
+
+        def round_and_quantize(name, raw, fmt, tag=None):
+            grouped = grouped_tile(name, tag)
+            mx = mx_tiles(name, K_PASS)
+            for runs in RUN_PAIRS:
+                round_by_query(grouped, nc.vector.tensor_copy, raw, runs=runs)
+            for runs in RUN_PAIRS:
+                quantize_runs(mx, grouped, runs, fmt)
+            return mx
 
         def grouped_tile(name, tag=None):
             return sbuf(name + "_grouped", [P, PACK, P, PACK], BF16, tag=tag)
@@ -155,7 +172,7 @@ def tile_attend_gat_lse_k_kernel(
         def weigh(g, q_mx, index, tag=None, rounds=1):
             weights[g, index] = sbuf("weights%d_%d" % (g, index), [P, PACK, HALF], F32, tag=tag)
             moving = (k_listed_codes[index], k_listed_scales[K_PLANE:, HALVES[index]])
-            scores = [bank(t) for t in range(PACK)]
+            scores = [bank(PACK * index + t) for t in range(PACK)]
             width = HALF // rounds
             for first in range(0, HALF, width):
                 for t in range(PACK):
@@ -181,18 +198,24 @@ def tile_attend_gat_lse_k_kernel(
         def ds_quantize(g, part, ds):
             quantize(ds_mx[g], part, ds[:].rearrange("p i t -> p (i t)"), E5M2)
 
-        def round_qm(m, raw, raw_block, copy, tag=None):
-            grouped = sbuf("qm_grouped%d" % m, [P, PASSES, P, PACK], BF16, tag=tag)
-            for g in range(PASSES):
-                copy(
-                    grouped[:, g, :, :].rearrange("p (c i) t -> p c t i", i=4),
-                    raw[g][:, :, raw_block * P : (raw_block + 1) * P].rearrange("p t (c i) -> p c t i", i=4),
-                )
-            return grouped
+        qm_grouped, qm_mx = {}, {}
 
-        def quantize_qm(grouped, mx, first_run):
-            columns = slice(first_run * P, (first_run + PASSES) * P)
-            quantize(mx, columns, grouped[:].rearrange("p g d t -> p (g d t)"), E4M3)
+        def qm_block(m, g):
+            raw = qm_raw_first if m < 2 else qm_raw_later
+            return raw[g][:, :, m % 2 * P : (m % 2 + 1) * P]
+
+        def round_qm(m, g, copy, grouped=None):
+            if grouped is None:
+                grouped = sbuf("qm_grouped%d_%d" % (m, g), [P, P, PACK], BF16)
+            qm_grouped[m, g] = grouped
+            copy(
+                qm_grouped[m, g][:].rearrange("p (c i) t -> p c t i", i=4),
+                qm_block(m, g).rearrange("p t (c i) -> p c t i", i=4),
+            )
+
+        def quantize_qm(m, g):
+            qm_mx[m, g] = mx_tiles("qm%d_%d" % (m, g), P)
+            quantize(qm_mx[m, g], slice(0, P), qm_grouped[m, g][:].rearrange("p d t -> p (d t)"), E4M3)
 
         by_scalar, by_vector = nc.scalar.copy, nc.vector.tensor_copy
 
@@ -207,13 +230,9 @@ def tile_attend_gat_lse_k_kernel(
         nc.scalar.mul(neg_lse[:], lse_q, -1.0)
         k_listed_scales = gather("k_scales", k_pool_scales, U8)
         gate(0, do_mx)
-        do_grouped = grouped_tile("do1", tag="k_pool_scales")
-        round_by_query(do_grouped, by_vector, do_raw[1])
-        gate(1, quantize_by_query("do1", do_grouped, E5M2))
+        gate(1, round_and_quantize("do1", do_raw[1], E5M2, tag="k_pool_scales"))
 
-        q_grouped = grouped_tile("q0")
-        round_by_query(q_grouped, by_vector, q_raw[0])
-        q_mx = quantize_by_query("q0", q_grouped, E4M3)
+        q_mx = round_and_quantize("q0", q_raw[0], E4M3)
         k_listed_codes = [gather("k_codes%d" % half.start, k_pool_words, U32, half) for half in HALVES]
         weigh(0, q_mx, 0, rounds=2)
         weigh(0, q_mx, 1)
@@ -221,81 +240,73 @@ def tile_attend_gat_lse_k_kernel(
         q_grouped = grouped_tile("q1")
         round_by_query(q_grouped, by_vector, q_raw[1][0], slice(0, P // 2))
         first_quarter = ds_product(0, QUARTERS[0], tag="q_raw1_0")
-        round_by_query(q_grouped, by_vector, q_raw[1][1], slice(P // 2, P))
+        for runs in RUN_PAIRS:
+            round_by_query(q_grouped, by_vector, q_raw[1][1], slice(P // 2, P), runs)
+        q_mx = mx_tiles("q1", K_PASS)
+        quantize_runs(q_mx, q_grouped, RUN_PAIRS[0], E4M3)
         ds_quantize(0, QUARTERS[0], first_quarter)
-        q_mx = quantize_by_query("q1", q_grouped, E4M3)
+        quantize_runs(q_mx, q_grouped, RUN_PAIRS[1], E4M3)
         weigh(1, q_mx, 0)
-        qm_first_grouped = round_qm(0, qm_raw_first, 0, by_scalar)
-        weigh(1, q_mx, 1, tag="qm_raw_first1")
+        for g in range(PASSES):
+            round_qm(0, g, by_scalar)
+        weigh(1, q_mx, 1)
+
+        def key_gradient(m, part):
+            acc = bank(2 * m + part.start // HALF)[:, 0 : part.stop - part.start]
+            for g in range(PASSES):
+                moving = [tile[:, part] for tile in ds_mx[g]]
+                multiply(acc, qm_mx[m, g], 0, E4M3, moving, E5M2, g == 0, g == PASSES - 1)
+            return acc
+
+        def dk_out(m, part, copy):
+            dk = sbuf("dk%d_%d" % (m, part.start), [P, part.stop - part.start], F32)
+            copy(dk[:], key_gradient(m, part))
+            return dk
+
+        def scatter_by_vector(m, part, dk):
+            nc.vector.tensor_copy(windows[m][:].indirect(entries(part)), dk[:])
+
+        def scatter_by_scalar(m, part, dk):
+            nc.scalar.activation(windows[m][:].indirect(entries(part)), dk[:], ACT.Copy)
+
+        def store(m):
+            nc.sync.dma_start(out[m * P : (m + 1) * P, :], windows[m][:])
+
+        def place_block(m):
+            for half in HALVES:
+                scatter_by_scalar(m, half, dk_out(m, half, by_scalar))
+            store(m)
+
         second_quarter = ds_product(0, QUARTERS[1])
         second_half = ds_product(0, HALVES[1])
         ds_quantize(0, QUARTERS[1], second_quarter)
         first_half = ds_product(1, HALVES[0])
-        ds_quantize(0, HALVES[1], second_half)
-        qm_first = mx_tiles("qm_first", PASSES * P)
-        quantize_qm(qm_first_grouped, qm_first, 0)
+        quantize_qm(0, 0)
+        quantize_qm(0, 1)
         ds_quantize(1, HALVES[0], first_half)
-
-        def key_gradient(m, index, qm_mx, first_run):
-            acc = bank((PACK + 2 * m + index) % (2 * PACK))[:, 0:HALF]
-            for g in range(PASSES):
-                moving = [tile[:, HALVES[index]] for tile in ds_mx[g]]
-                multiply(acc, qm_mx, first_run + g, E4M3, moving, E5M2, g == 0, g == PASSES - 1)
-            return acc
-
-        def copy_out(m, index, acc, copy):
-            dk = sbuf("dk%d_%d" % (m, index), [P, HALF], F32)
-            copy(dk[:], acc)
-            return dk
-
-        def scatter_by_vector(m, index, dk):
-            nc.vector.tensor_copy(windows[m % WINDOWS][:].indirect(entries(HALVES[index])), dk[:])
-
-        def scatter_by_scalar(m, index, dk):
-            nc.scalar.activation(windows[m % WINDOWS][:].indirect(entries(HALVES[index])), dk[:], ACT.Copy)
-
-        def store(m):
-            nc.sync.dma_start(out[m * P : (m + 1) * P, :], windows[m % WINDOWS][:])
-
-        first_dk = copy_out(0, 0, key_gradient(0, 0, qm_first, 0), by_scalar)
-        scatter_by_scalar(0, 0, first_dk)
+        ds_quantize(0, HALVES[1], second_half)
+        second_block = sbuf("qm_grouped1", [P, PASSES, P, PACK], BF16, tag="neg_lse")
+        for g in range(PASSES):
+            round_qm(1, g, by_scalar, second_block[:, g])
+        scatter_by_scalar(0, HALVES[0], dk_out(0, HALVES[0], by_scalar))
         third_quarter = ds_product(1, QUARTERS[2])
         last_quarter = ds_product(1, QUARTERS[3])
         ds_quantize(1, QUARTERS[2], third_quarter)
+        quantize_qm(1, 0)
         ds_quantize(1, QUARTERS[3], last_quarter)
-        last_dk = copy_out(0, 1, key_gradient(0, 1, qm_first, 0), by_scalar)
-
-        qm_later = mx_tiles("qm_later", (D_TILES - 1) * PASSES * P)
-
-        def round_later(m):
-            return round_qm(m, qm_raw_later, m - 1, by_vector)
-
-        def quantize_later(m, g, grouped):
-            run = (m - 1) * PASSES + g
-            quantize(qm_later, slice(run * P, (run + 1) * P), grouped[:, g].rearrange("p d t -> p (d t)"), E4M3)
-
-        def later_dk(m, index, copy):
-            return copy_out(m, index, key_gradient(m, index, qm_later, (m - 1) * PASSES), copy)
-
-        def place_block(m):
-            for index in range(len(HALVES)):
-                scatter_by_scalar(m, index, later_dk(m, index, by_scalar))
-            store(m)
-
-        second_grouped = round_later(1)
-        quantize_later(1, 0, second_grouped)
-        third_grouped = round_later(2)
-        quantize_later(1, 1, second_grouped)
+        quantize_qm(1, 1)
+        for m in (2, 3):
+            for g in range(PASSES):
+                round_qm(m, g, by_vector)
         for g in range(PASSES):
-            quantize_later(2, g, third_grouped)
-        scatter_by_vector(0, 1, last_dk)
+            quantize_qm(2, g)
+        last_dk = dk_out(0, HALVES[1], by_vector)
+        quantize_qm(3, 0)
+        scatter_by_vector(0, HALVES[1], last_dk)
         store(0)
         place_block(1)
-        last_grouped = round_later(3)
-        dk = later_dk(2, 0, by_vector)
-        for g in range(PASSES):
-            quantize_later(3, g, last_grouped)
-        scatter_by_vector(2, 0, dk)
-        scatter_by_vector(2, 1, later_dk(2, 1, by_scalar))
+        dk = dk_out(2, slice(0, N), by_vector)
+        quantize_qm(3, 1)
+        scatter_by_vector(2, slice(0, N), dk)
         store(2)
         place_block(3)

@@ -220,9 +220,12 @@ def tile_attend_gat_lse_k_kernel(
         by_scalar, by_vector = nc.scalar.copy, nc.vector.tensor_copy
 
         do_grouped = grouped_tile("do0")
-        round_by_query(do_grouped, by_scalar, do_raw[0])
+        for runs in RUN_PAIRS:
+            round_by_query(do_grouped, by_scalar, do_raw[0], runs=runs)
         v_listed_scales = gather("v_scales", v_pool_scales, U8)
-        do_mx = quantize_by_query("do0", do_grouped, E5M2, tag="v_pool_scales")
+        do_mx = mx_tiles("do0", K_PASS, tag="v_pool_scales")
+        for runs in RUN_PAIRS:
+            quantize_runs(do_mx, do_grouped, runs, E5M2)
         values = (gather("v_codes", v_pool_words, U32), v_listed_scales)
         neg_delta_rw = sbuf("neg_delta_rw", [P, PASSES, PACK], F32)
         nc.vector.scalar_tensor_tensor(neg_delta_rw[:], delta_q, -1.0, rw_q, ALU.mult, ALU.mult)
@@ -238,7 +241,8 @@ def tile_attend_gat_lse_k_kernel(
         weigh(0, q_mx, 1)
 
         q_grouped = grouped_tile("q1")
-        round_by_query(q_grouped, by_vector, q_raw[1][0], slice(0, P // 2))
+        for runs in RUN_PAIRS:
+            round_by_query(q_grouped, by_vector, q_raw[1][0], slice(0, P // 2), runs)
         first_quarter = ds_product(0, QUARTERS[0], tag="q_raw1_0")
         for runs in RUN_PAIRS:
             round_by_query(q_grouped, by_vector, q_raw[1][1], slice(P // 2, P), runs)

@@ -27,6 +27,10 @@ QUARTERS = tuple(slice(c * N // 4, (c + 1) * N // 4) for c in range(4))
 RUN_PAIRS = (slice(0, 2), slice(2, PACK))
 K_PLANE = 4
 PLACES = {
+    "window3": 16896, "v_pool_scales": 24576, "do_raw1": 61440, "q_raw1_0": 61440, "q_raw1_256": 65536, "ds0_0": 61440,
+    "q_raw0": 33792, "qm_raw_first0": 33792, "qm_raw_first1": 37888, "k_pool_scales": 41472,
+    "k_pool_words": 42496, "qm_raw_later0": 42496, "qm_raw_later1": 46592,
+    "v_pool_words": 53248, "lse_q": 53248,
     "q1_grouped": 0, "ds0_128": 0, "ds0_256": 1024,
     "dk0_256": 4096, "qm3_1_codes": 4096,
     "gated1": 8192, "qm_grouped2_0": 8192, "qm_grouped2_1": 9216, "qm_grouped3_0": 10240, "dk1_256": 10240, "qm_grouped3_1": 11264,
@@ -55,8 +59,12 @@ def tile_attend_gat_lse_k_kernel(
         nc.gpsimd.memset(v_pool_scales[:], 0)
         k_pool_scales = sbuf("k_pool_scales", [P, T // 4], I32)
         nc.vector.memset(k_pool_scales[:], 0)
+        v_plane = sbuf("v_plane", [P, N], U8)
+        k_plane = sbuf("k_plane", [P, N], U8)
+        for plane in (v_plane, k_plane):
+            nc.gpsimd.memset(plane[:].bitcast(I32), 0)
 
-        windows = [sbuf("window%d" % w, [P, T], F32) for w in range(WINDOWS)]
+        windows = [sbuf("window%d" % w, [P, T], F32) for w in range(WINDOWS - 1)]
         for window in windows:
             nc.vector.memset(window[:], 0.0)
 
@@ -78,9 +86,22 @@ def tile_attend_gat_lse_k_kernel(
             nc.sync.dma_start(pool_words[:], words[0].rearrange("p t j -> p (t j)").bitcast(I32))
             return pool_words
 
-        def load_pool_scales(pool_scales, scales, rows, first=0):
-            for row in rows:
-                nc.sync.dma_start(pool_scales[first + row : P : 32, :], scales[0, row:16:4, :].bitcast(I32))
+        def load_pool_scales(pool_scales, scales, first):
+            nc.sync.dma_start(pool_scales[first:P:8, :], scales[0].bitcast(I32))
+
+        def move_to_plane(plane, listed, first):
+            for row in range(4):
+                nc.sync.dma_start(
+                    plane[first + row : P : 32, :].bitcast(I32), listed[first + 8 * row : P : 32, :].bitcast(I32)
+                )
+
+        def entries(part):
+            return offsets[:, part.start // 16 : part.stop // 16]
+
+        def gather(name, window, dtype, part=slice(0, N)):
+            listed = sbuf(name, [P, part.stop - part.start], dtype)
+            nc.vector.tensor_copy(listed[:], window[:].bitcast(dtype).indirect(entries(part)))
+            return listed
 
         def queries(g):
             return slice(g * K_PASS, (g + 1) * K_PASS)
@@ -90,26 +111,23 @@ def tile_attend_gat_lse_k_kernel(
         nc.sync.dma_start(offsets[:], offs)
         delta_q = load_per_query("delta_q", delta)
         rw_q = load_per_query("rw_q", rw)
-        lse_q = load_per_query("lse_q", lse)
-        do_raw[0] = load_rows("do_raw0", doT[0, :, queries(0)], pieces=2)
-        load_pool_scales(v_pool_scales, v_scales, range(4))
-        load_pool_scales(k_pool_scales, k_scales, range(2), K_PLANE)
+        do_raw[0] = sbuf("do_raw0", [P, PACK, K_PASS], F32)
+        do_rows = doT[0, :, queries(0)].rearrange("(p j) c -> p j c", j=PACK)
+        for j in range(PACK - 1):
+            nc.sync.dma_start(do_raw[0][:, j, :], do_rows[:, j, :])
+        load_pool_scales(v_pool_scales, v_scales, 0)
+        load_pool_scales(k_pool_scales, k_scales, K_PLANE)
+        nc.sync.dma_start(do_raw[0][:, PACK - 1, :], do_rows[:, PACK - 1, :])
         v_pool_words = load_pool_words("v_pool_words", v_words)
-        load_pool_scales(k_pool_scales, k_scales, range(2, 4), K_PLANE)
         do_raw[1] = load_rows("do_raw1", doT[0, :, queries(1)])
+        move_to_plane(v_plane, gather("v_scales", v_pool_scales, U8), 0)
+        k_listed_scales = gather("k_scales", k_pool_scales, U8)
+        last_window = sbuf("window3", [P, T], F32)
+        nc.vector.memset(last_window[:], 0.0)
+        windows.append(last_window)
         q_raw[0] = load_rows("q_raw0", qT[0, :, queries(0)])
+        move_to_plane(k_plane, k_listed_scales, K_PLANE)
         k_pool_words = load_pool_words("k_pool_words", k_words)
-        q_raw[1] = [load_rows("q_raw1_%d" % half.start, qT[0, :, queries(1)][:, half]) for half in HALVES]
-        qm_raw_first = [load_rows("qm_raw_first%d" % g, qm[0, queries(g), 0 : D // 2]) for g in range(PASSES)]
-        qm_raw_later = [load_rows("qm_raw_later%d" % g, qm[0, queries(g), D // 2 : D]) for g in range(PASSES)]
-
-        def entries(part):
-            return offsets[:, part.start // 16 : part.stop // 16]
-
-        def gather(name, window, dtype, part=slice(0, N)):
-            listed = sbuf(name, [P, part.stop - part.start], dtype)
-            nc.vector.tensor_copy(listed[:], window[:].bitcast(dtype).indirect(entries(part)))
-            return listed
 
         def mx_tiles(name, width, tag=None):
             return sbuf(name + "_codes", [P, width], U32, tag=tag), sbuf(name + "_scales", [P, width], U8)
@@ -171,7 +189,7 @@ def tile_attend_gat_lse_k_kernel(
 
         def weigh(g, q_mx, index, tag=None, rounds=1):
             weights[g, index] = sbuf("weights%d_%d" % (g, index), [P, PACK, HALF], F32, tag=tag)
-            moving = (k_listed_codes[index], k_listed_scales[K_PLANE:, HALVES[index]])
+            moving = (k_listed_codes[index], k_plane[K_PLANE:, HALVES[index]])
             scores = [bank(PACK * index + t) for t in range(PACK)]
             width = HALF // rounds
             for first in range(0, HALF, width):
@@ -222,28 +240,30 @@ def tile_attend_gat_lse_k_kernel(
         do_grouped = grouped_tile("do0")
         for runs in RUN_PAIRS:
             round_by_query(do_grouped, by_scalar, do_raw[0], runs=runs)
-        v_listed_scales = gather("v_scales", v_pool_scales, U8)
-        do_mx = mx_tiles("do0", K_PASS, tag="v_pool_scales")
+        do_mx = mx_tiles("do0", K_PASS)
         for runs in RUN_PAIRS:
             quantize_runs(do_mx, do_grouped, runs, E5M2)
-        values = (gather("v_codes", v_pool_words, U32), v_listed_scales)
+        values = (gather("v_codes", v_pool_words, U32), v_plane)
+        lse_q = load_per_query("lse_q", lse)
         neg_delta_rw = sbuf("neg_delta_rw", [P, PASSES, PACK], F32)
         nc.vector.scalar_tensor_tensor(neg_delta_rw[:], delta_q, -1.0, rw_q, ALU.mult, ALU.mult)
-        neg_lse = sbuf("neg_lse", [P, PASSES, PACK], F32)
-        nc.scalar.mul(neg_lse[:], lse_q, -1.0)
-        k_listed_scales = gather("k_scales", k_pool_scales, U8)
         gate(0, do_mx)
-        gate(1, round_and_quantize("do1", do_raw[1], E5M2, tag="k_pool_scales"))
+        gate(1, round_and_quantize("do1", do_raw[1], E5M2))
+        q_raw[1] = [load_rows("q_raw1_%d" % half.start, qT[0, :, queries(1)][:, half]) for half in HALVES]
 
         q_mx = round_and_quantize("q0", q_raw[0], E4M3)
+        qm_raw_first = [load_rows("qm_raw_first%d" % g, qm[0, queries(g), 0 : D // 2]) for g in range(PASSES)]
         k_listed_codes = [gather("k_codes%d" % half.start, k_pool_words, U32, half) for half in HALVES]
+        qm_raw_later = [load_rows("qm_raw_later%d" % g, qm[0, queries(g), D // 2 : D]) for g in range(PASSES)]
+        neg_lse = sbuf("neg_lse", [P, PASSES, PACK], F32)
+        nc.scalar.mul(neg_lse[:], lse_q, -1.0)
         weigh(0, q_mx, 0, rounds=2)
         weigh(0, q_mx, 1)
 
         q_grouped = grouped_tile("q1")
         for runs in RUN_PAIRS:
             round_by_query(q_grouped, by_vector, q_raw[1][0], slice(0, P // 2), runs)
-        first_quarter = ds_product(0, QUARTERS[0], tag="q_raw1_0")
+        first_quarter = ds_product(0, QUARTERS[0])
         for runs in RUN_PAIRS:
             round_by_query(q_grouped, by_vector, q_raw[1][1], slice(P // 2, P), runs)
         q_mx = mx_tiles("q1", K_PASS)

@@ -26,16 +26,21 @@ HALVES = (slice(0, HALF), slice(HALF, N))
 QUARTERS = tuple(slice(c * N // 4, (c + 1) * N // 4) for c in range(4))
 RUN_PAIRS = (slice(0, 2), slice(2, PACK))
 K_PLANE = 4
+SPREAD = P // 16
+KB = 1024
 PLACES = {
-    "window3": 16896, "v_pool_scales": 24576, "do_raw1": 61440, "q_raw1_0": 61440, "q_raw1_256": 65536, "ds0_0": 61440,
-    "q_raw0": 33792, "qm_raw_first0": 33792, "qm_raw_first1": 37888, "k_pool_scales": 41472,
-    "k_pool_words": 42496, "qm_raw_later0": 42496, "qm_raw_later1": 46592,
-    "v_pool_words": 53248, "lse_q": 53248,
-    "q1_grouped": 0, "ds0_128": 0, "ds0_256": 1024,
-    "dk0_256": 4096, "qm3_1_codes": 4096,
-    "gated1": 8192, "qm_grouped2_0": 8192, "qm_grouped2_1": 9216, "qm_grouped3_0": 10240, "dk1_256": 10240, "qm_grouped3_1": 11264,
+    "q1_grouped": 0, "ds0_128": 0, "ds0_256": 1 * KB,
+    "dk0_256": 4 * KB, "qm3_1_codes": 4 * KB,
+    "gated1": 8 * KB,
+    "qm_grouped2_0": 8 * KB, "qm_grouped2_1": 9 * KB, "qm_grouped3_0": 10 * KB, "qm_grouped3_1": 11 * KB,
+    "dk1_256": 10 * KB,
+    "q_raw0": 33 * KB, "k_pool_scales": 40 * KB + KB // 2, "k_pool_words": 41 * KB + KB // 2,
+    "v_pool_words": 52 * KB, "lse_q": 52 * KB,
+    "do_raw1": 60 * KB, "q_raw1_0": 60 * KB, "q_raw1_256": 64 * KB,
+    "qm_raw_first0": 33 * KB, "qm_raw_first1": 37 * KB,
+    "qm_raw_later0": 41 * KB + KB // 2, "qm_raw_later1": 45 * KB + KB // 2,
+    "ds0_0": 60 * KB,
 }
-WINDOWS = 4
 
 
 def tile_attend_gat_lse_k_kernel(
@@ -64,16 +69,16 @@ def tile_attend_gat_lse_k_kernel(
         for plane in (v_plane, k_plane):
             nc.gpsimd.memset(plane[:].bitcast(I32), 0)
 
-        windows = [sbuf("window%d" % w, [P, T], F32) for w in range(WINDOWS - 1)]
+        windows = [sbuf("window%d" % m, [P, T], F32) for m in range(D_TILES)]
         for window in windows:
             nc.vector.memset(window[:], 0.0)
 
-        def load_rows(name, rows, pieces=1):
+        def by_partition(rows):
+            return rows.rearrange("(p j) c -> p j c", j=PACK)
+
+        def load_rows(name, rows):
             raw = sbuf(name, [P, PACK, rows.shape[1]], F32)
-            by_partition = rows.rearrange("(p j) c -> p j c", j=PACK)
-            step = PACK // pieces
-            for j in range(0, PACK, step):
-                nc.sync.dma_start(raw[:, j : j + step, :], by_partition[:, j : j + step, :])
+            nc.sync.dma_start(raw[:], by_partition(rows))
             return raw
 
         def load_per_query(name, values):
@@ -87,12 +92,13 @@ def tile_attend_gat_lse_k_kernel(
             return pool_words
 
         def load_pool_scales(pool_scales, scales, first):
-            nc.sync.dma_start(pool_scales[first:P:8, :], scales[0].bitcast(I32))
+            nc.sync.dma_start(pool_scales[first:P:SPREAD, :], scales[0].bitcast(I32))
 
         def move_to_plane(plane, listed, first):
             for row in range(4):
                 nc.sync.dma_start(
-                    plane[first + row : P : 32, :].bitcast(I32), listed[first + 8 * row : P : 32, :].bitcast(I32)
+                    plane[first + row : P : 32, :].bitcast(I32),
+                    listed[first + SPREAD * row : P : 32, :].bitcast(I32),
                 )
 
         def entries(part):
@@ -112,7 +118,7 @@ def tile_attend_gat_lse_k_kernel(
         delta_q = load_per_query("delta_q", delta)
         rw_q = load_per_query("rw_q", rw)
         do_raw[0] = sbuf("do_raw0", [P, PACK, K_PASS], F32)
-        do_rows = doT[0, :, queries(0)].rearrange("(p j) c -> p j c", j=PACK)
+        do_rows = by_partition(doT[0, :, queries(0)])
         for j in range(PACK - 1):
             nc.sync.dma_start(do_raw[0][:, j, :], do_rows[:, j, :])
         load_pool_scales(v_pool_scales, v_scales, 0)
@@ -122,44 +128,31 @@ def tile_attend_gat_lse_k_kernel(
         do_raw[1] = load_rows("do_raw1", doT[0, :, queries(1)])
         move_to_plane(v_plane, gather("v_scales", v_pool_scales, U8), 0)
         k_listed_scales = gather("k_scales", k_pool_scales, U8)
-        last_window = sbuf("window3", [P, T], F32)
-        nc.vector.memset(last_window[:], 0.0)
-        windows.append(last_window)
         q_raw[0] = load_rows("q_raw0", qT[0, :, queries(0)])
-        move_to_plane(k_plane, k_listed_scales, K_PLANE)
         k_pool_words = load_pool_words("k_pool_words", k_words)
+        move_to_plane(k_plane, k_listed_scales, K_PLANE)
 
-        def mx_tiles(name, width, tag=None):
-            return sbuf(name + "_codes", [P, width], U32, tag=tag), sbuf(name + "_scales", [P, width], U8)
+        def mx_tiles(name, width):
+            return sbuf(name + "_codes", [P, width], U32), sbuf(name + "_scales", [P, width], U8)
 
         def quantize(mx, columns, grouped, fmt):
             nc.vector.quantize_mx(out=mx[0][:, columns].bitcast(fmt), scales=mx[1][:, columns], in_=grouped)
 
-        def round_by_query(grouped, copy, raw, m_range=slice(0, P), runs=slice(0, PACK)):
-            copy(
-                grouped[:].rearrange("p t m j -> p m j t")[:, m_range, :, runs],
-                raw[:].rearrange("p j (m t) -> p m j t", t=PACK)[:, :, :, runs],
-            )
+        def grouped_tile(name):
+            return sbuf(name + "_grouped", [P, PACK, P, PACK], BF16)
 
-        def quantize_runs(mx, grouped, runs, fmt):
-            columns = slice(runs.start * P, runs.stop * P)
-            quantize(mx, columns, grouped[:, runs].rearrange("p t m j -> p (t m j)"), fmt)
+        def round_by_query(grouped, copy, raw, m_range=slice(0, P)):
+            for runs in RUN_PAIRS:
+                copy(
+                    grouped[:].rearrange("p t m j -> p m j t")[:, m_range, :, runs],
+                    raw[:].rearrange("p j (m t) -> p m j t", t=PACK)[:, :, :, runs],
+                )
 
-        def round_and_quantize(name, raw, fmt, tag=None):
-            grouped = grouped_tile(name, tag)
+        def quantize_by_query(name, grouped, fmt):
             mx = mx_tiles(name, K_PASS)
             for runs in RUN_PAIRS:
-                round_by_query(grouped, nc.vector.tensor_copy, raw, runs=runs)
-            for runs in RUN_PAIRS:
-                quantize_runs(mx, grouped, runs, fmt)
-            return mx
-
-        def grouped_tile(name, tag=None):
-            return sbuf(name + "_grouped", [P, PACK, P, PACK], BF16, tag=tag)
-
-        def quantize_by_query(name, grouped, fmt, tag=None):
-            mx = mx_tiles(name, K_PASS, tag)
-            quantize(mx, slice(0, K_PASS), grouped[:].rearrange("p t m j -> p (t m j)"), fmt)
+                columns = slice(runs.start * P, runs.stop * P)
+                quantize(mx, columns, grouped[:, runs].rearrange("p t m j -> p (t m j)"), fmt)
             return mx
 
         def multiply(acc, stationary, run, stationary_fmt, moving, moving_fmt, start, stop):
@@ -187,8 +180,8 @@ def tile_attend_gat_lse_k_kernel(
                     bias=neg_delta_rw[:, g, t : t + 1], scale=rw_q[:, g, t : t + 1],
                 )
 
-        def weigh(g, q_mx, index, tag=None, rounds=1):
-            weights[g, index] = sbuf("weights%d_%d" % (g, index), [P, PACK, HALF], F32, tag=tag)
+        def weigh(g, q_mx, index, rounds=1):
+            weights[g, index] = sbuf("weights%d_%d" % (g, index), [P, PACK, HALF], F32)
             moving = (k_listed_codes[index], k_plane[K_PLANE:, HALVES[index]])
             scores = [bank(PACK * index + t) for t in range(PACK)]
             width = HALF // rounds
@@ -201,10 +194,10 @@ def tile_attend_gat_lse_k_kernel(
                         ACT.Exp, bias=neg_lse[:, g, t : t + 1],
                     )
 
-        def ds_product(g, part, tag=None):
+        def ds_product(g, part):
             width = part.stop - part.start
             index, first = divmod(part.start, HALF)
-            ds = sbuf("ds%d_%d" % (g, part.start), [P, width, PACK], BF16, tag=tag)
+            ds = sbuf("ds%d_%d" % (g, part.start), [P, width, PACK], BF16)
             nc.vector.tensor_tensor(
                 ds[:].rearrange("p (c i) t -> p c t i", i=2),
                 weights[g, index][:, :, first : first + width].rearrange("p t (c i) -> p c t i", i=2),
@@ -218,61 +211,56 @@ def tile_attend_gat_lse_k_kernel(
 
         qm_grouped, qm_mx = {}, {}
 
-        def qm_block(m, g):
-            raw = qm_raw_first if m < 2 else qm_raw_later
-            return raw[g][:, :, m % 2 * P : (m % 2 + 1) * P]
-
-        def round_qm(m, g, copy, grouped=None):
-            if grouped is None:
-                grouped = sbuf("qm_grouped%d_%d" % (m, g), [P, P, PACK], BF16)
+        def round_qm(m, g, copy, grouped):
+            half, block = divmod(m, D_TILES // 2)
             qm_grouped[m, g] = grouped
             copy(
-                qm_grouped[m, g][:].rearrange("p (c i) t -> p c t i", i=4),
-                qm_block(m, g).rearrange("p t (c i) -> p c t i", i=4),
+                grouped.rearrange("p (c i) t -> p c t i", i=4),
+                qm_raw[half][g][:, :, block * P : (block + 1) * P].rearrange("p t (c i) -> p c t i", i=4),
             )
+
+        def qm_piece(m, g):
+            return sbuf("qm_grouped%d_%d" % (m, g), [P, P, PACK], BF16)[:]
 
         def quantize_qm(m, g):
             qm_mx[m, g] = mx_tiles("qm%d_%d" % (m, g), P)
-            quantize(qm_mx[m, g], slice(0, P), qm_grouped[m, g][:].rearrange("p d t -> p (d t)"), E4M3)
+            quantize(qm_mx[m, g], slice(0, P), qm_grouped[m, g].rearrange("p d t -> p (d t)"), E4M3)
 
         by_scalar, by_vector = nc.scalar.copy, nc.vector.tensor_copy
 
         do_grouped = grouped_tile("do0")
-        for runs in RUN_PAIRS:
-            round_by_query(do_grouped, by_scalar, do_raw[0], runs=runs)
-        do_mx = mx_tiles("do0", K_PASS)
-        for runs in RUN_PAIRS:
-            quantize_runs(do_mx, do_grouped, runs, E5M2)
+        round_by_query(do_grouped, by_scalar, do_raw[0])
+        do_mx = quantize_by_query("do0", do_grouped, E5M2)
         values = (gather("v_codes", v_pool_words, U32), v_plane)
         lse_q = load_per_query("lse_q", lse)
         neg_delta_rw = sbuf("neg_delta_rw", [P, PASSES, PACK], F32)
         nc.vector.scalar_tensor_tensor(neg_delta_rw[:], delta_q, -1.0, rw_q, ALU.mult, ALU.mult)
         gate(0, do_mx)
-        gate(1, round_and_quantize("do1", do_raw[1], E5M2))
+        do_grouped = grouped_tile("do1")
+        round_by_query(do_grouped, by_vector, do_raw[1])
+        gate(1, quantize_by_query("do1", do_grouped, E5M2))
         q_raw[1] = [load_rows("q_raw1_%d" % half.start, qT[0, :, queries(1)][:, half]) for half in HALVES]
 
-        q_mx = round_and_quantize("q0", q_raw[0], E4M3)
-        qm_raw_first = [load_rows("qm_raw_first%d" % g, qm[0, queries(g), 0 : D // 2]) for g in range(PASSES)]
+        q_grouped = grouped_tile("q0")
+        round_by_query(q_grouped, by_vector, q_raw[0])
+        q_mx = quantize_by_query("q0", q_grouped, E4M3)
+        qm_raw = [[load_rows("qm_raw_first%d" % g, qm[0, queries(g), 0 : D // 2]) for g in range(PASSES)]]
         k_listed_codes = [gather("k_codes%d" % half.start, k_pool_words, U32, half) for half in HALVES]
-        qm_raw_later = [load_rows("qm_raw_later%d" % g, qm[0, queries(g), D // 2 : D]) for g in range(PASSES)]
+        qm_raw.append([load_rows("qm_raw_later%d" % g, qm[0, queries(g), D // 2 : D]) for g in range(PASSES)])
         neg_lse = sbuf("neg_lse", [P, PASSES, PACK], F32)
         nc.scalar.mul(neg_lse[:], lse_q, -1.0)
         weigh(0, q_mx, 0, rounds=2)
         weigh(0, q_mx, 1)
 
         q_grouped = grouped_tile("q1")
-        for runs in RUN_PAIRS:
-            round_by_query(q_grouped, by_vector, q_raw[1][0], slice(0, P // 2), runs)
+        round_by_query(q_grouped, by_vector, q_raw[1][0], slice(0, P // 2))
         first_quarter = ds_product(0, QUARTERS[0])
-        for runs in RUN_PAIRS:
-            round_by_query(q_grouped, by_vector, q_raw[1][1], slice(P // 2, P), runs)
-        q_mx = mx_tiles("q1", K_PASS)
-        quantize_runs(q_mx, q_grouped, RUN_PAIRS[0], E4M3)
+        round_by_query(q_grouped, by_vector, q_raw[1][1], slice(P // 2, P))
+        q_mx = quantize_by_query("q1", q_grouped, E4M3)
         ds_quantize(0, QUARTERS[0], first_quarter)
-        quantize_runs(q_mx, q_grouped, RUN_PAIRS[1], E4M3)
         weigh(1, q_mx, 0)
         for g in range(PASSES):
-            round_qm(0, g, by_scalar)
+            round_qm(0, g, by_scalar, qm_piece(0, g))
         weigh(1, q_mx, 1)
 
         def key_gradient(m, part):
@@ -296,7 +284,7 @@ def tile_attend_gat_lse_k_kernel(
         def store(m):
             nc.sync.dma_start(out[m * P : (m + 1) * P, :], windows[m][:])
 
-        def place_block(m):
+        def place_by_scalar(m):
             for half in HALVES:
                 scatter_by_scalar(m, half, dk_out(m, half, by_scalar))
             store(m)
@@ -305,8 +293,8 @@ def tile_attend_gat_lse_k_kernel(
         second_half = ds_product(0, HALVES[1])
         ds_quantize(0, QUARTERS[1], second_quarter)
         first_half = ds_product(1, HALVES[0])
-        quantize_qm(0, 0)
-        quantize_qm(0, 1)
+        for g in range(PASSES):
+            quantize_qm(0, g)
         ds_quantize(1, HALVES[0], first_half)
         ds_quantize(0, HALVES[1], second_half)
         second_block = sbuf("qm_grouped1", [P, PASSES, P, PACK], BF16, tag="neg_lse")
@@ -319,18 +307,19 @@ def tile_attend_gat_lse_k_kernel(
         quantize_qm(1, 0)
         ds_quantize(1, QUARTERS[3], last_quarter)
         quantize_qm(1, 1)
-        for m in (2, 3):
+
+        for m in range(D_TILES // 2, D_TILES):
             for g in range(PASSES):
-                round_qm(m, g, by_vector)
+                round_qm(m, g, by_vector, qm_piece(m, g))
         for g in range(PASSES):
             quantize_qm(2, g)
         last_dk = dk_out(0, HALVES[1], by_vector)
         quantize_qm(3, 0)
         scatter_by_vector(0, HALVES[1], last_dk)
         store(0)
-        place_block(1)
+        place_by_scalar(1)
         dk = dk_out(2, slice(0, N), by_vector)
         quantize_qm(3, 1)
         scatter_by_vector(2, slice(0, N), dk)
         store(2)
-        place_block(3)
+        place_by_scalar(3)

@@ -34,11 +34,12 @@ PLACES = {
     "gated1": 8 * KB,
     "qm_grouped2_0": 8 * KB, "qm_grouped2_1": 9 * KB, "qm_grouped3_0": 10 * KB, "qm_grouped3_1": 11 * KB,
     "dk1_256": 10 * KB,
-    "q_raw0": 33 * KB, "k_pool_scales": 40 * KB + KB // 2, "k_pool_words": 41 * KB + KB // 2,
+    "window3": 16 * KB + KB // 2, "v_pool_scales": 24 * KB,
+    "q_raw0": 25 * KB, "k_pool_scales": 41 * KB, "k_pool_words": 41 * KB,
     "v_pool_words": 52 * KB, "lse_q": 52 * KB,
     "do_raw1": 60 * KB, "q_raw1_0": 60 * KB, "q_raw1_256": 64 * KB,
-    "qm_raw_first0": 33 * KB, "qm_raw_first1": 37 * KB,
-    "qm_raw_later0": 41 * KB + KB // 2, "qm_raw_later1": 45 * KB + KB // 2,
+    "qm_raw_first0": 25 * KB, "qm_raw_first1": 29 * KB,
+    "qm_raw_later0": 41 * KB, "qm_raw_later1": 45 * KB,
     "ds0_0": 60 * KB,
 }
 
@@ -69,9 +70,12 @@ def tile_attend_gat_lse_k_kernel(
         for plane in (v_plane, k_plane):
             nc.gpsimd.memset(plane[:].bitcast(I32), 0)
 
-        windows = [sbuf("window%d" % m, [P, T], F32) for m in range(D_TILES)]
-        for window in windows:
+        def zeroed_window(m):
+            window = sbuf("window%d" % m, [P, T], F32)
             nc.vector.memset(window[:], 0.0)
+            return window
+
+        windows = [zeroed_window(m) for m in range(D_TILES - 1)]
 
         def by_partition(rows):
             return rows.rearrange("(p j) c -> p j c", j=PACK)
@@ -128,9 +132,10 @@ def tile_attend_gat_lse_k_kernel(
         do_raw[1] = load_rows("do_raw1", doT[0, :, queries(1)])
         move_to_plane(v_plane, gather("v_scales", v_pool_scales, U8), 0)
         k_listed_scales = gather("k_scales", k_pool_scales, U8)
+        windows.append(zeroed_window(D_TILES - 1))
         q_raw[0] = load_rows("q_raw0", qT[0, :, queries(0)])
-        k_pool_words = load_pool_words("k_pool_words", k_words)
         move_to_plane(k_plane, k_listed_scales, K_PLANE)
+        k_pool_words = load_pool_words("k_pool_words", k_words)
 
         def mx_tiles(name, width):
             return sbuf(name + "_codes", [P, width], U32), sbuf(name + "_scales", [P, width], U8)

@@ -38,8 +38,8 @@ PLACES = {
     "q_raw0": 25 * KB, "k_pool_scales": 41 * KB, "k_pool_words": 41 * KB,
     "v_pool_words": 52 * KB, "lse_q": 52 * KB,
     "do_raw1": 60 * KB, "q_raw1_0": 60 * KB, "q_raw1_256": 64 * KB,
-    "qm_raw_first0": 25 * KB, "qm_raw_first1": 29 * KB,
-    "qm_raw_later0": 41 * KB, "qm_raw_later1": 45 * KB,
+    "qm_raw_first1": 25 * KB, "qm_raw0_0": 31 * KB, "weights1_0": 31 * KB,
+    "qm_raw_later0": 41 * KB, "qm_raw_later1": 47 * KB,
     "ds0_0": 60 * KB,
 }
 
@@ -217,11 +217,10 @@ def tile_attend_gat_lse_k_kernel(
         qm_grouped, qm_mx = {}, {}
 
         def round_qm(m, g, copy, grouped):
-            half, block = divmod(m, D_TILES // 2)
             qm_grouped[m, g] = grouped
             copy(
                 grouped.rearrange("p (c i) t -> p c t i", i=4),
-                qm_raw[half][g][:, :, block * P : (block + 1) * P].rearrange("p t (c i) -> p c t i", i=4),
+                qm_raw[m, g].rearrange("p t (c i) -> p c t i", i=4),
             )
 
         def qm_piece(m, g):
@@ -249,9 +248,14 @@ def tile_attend_gat_lse_k_kernel(
         q_grouped = grouped_tile("q0")
         round_by_query(q_grouped, by_vector, q_raw[0])
         q_mx = quantize_by_query("q0", q_grouped, E4M3)
-        qm_raw = [[load_rows("qm_raw_first%d" % g, qm[0, queries(g), 0 : D // 2]) for g in range(PASSES)]]
+        qm_raw = {(0, 0): load_rows("qm_raw0_0", qm[0, queries(0), 0:P])[:]}
+        first = load_rows("qm_raw_first1", qm[0, queries(1), 0 : D // 2])
+        qm_raw.update({(m, 1): first[:, :, m * P : (m + 1) * P] for m in range(2)})
         k_listed_codes = [gather("k_codes%d" % half.start, k_pool_words, U32, half) for half in HALVES]
-        qm_raw.append([load_rows("qm_raw_later%d" % g, qm[0, queries(g), D // 2 : D]) for g in range(PASSES)])
+        for g in range(PASSES):
+            done = 1 + g
+            later = load_rows("qm_raw_later%d" % g, qm[0, queries(g), done * P : D])
+            qm_raw.update({(m, g): later[:, :, (m - done) * P : (m - done + 1) * P] for m in range(done, D_TILES)})
         neg_lse = sbuf("neg_lse", [P, PASSES, PACK], F32)
         nc.scalar.mul(neg_lse[:], lse_q, -1.0)
         weigh(0, q_mx, 0, rounds=2)
@@ -263,9 +267,9 @@ def tile_attend_gat_lse_k_kernel(
         round_by_query(q_grouped, by_vector, q_raw[1][1], slice(P // 2, P))
         q_mx = quantize_by_query("q1", q_grouped, E4M3)
         ds_quantize(0, QUARTERS[0], first_quarter)
+        round_qm(0, 0, by_scalar, qm_piece(0, 0))
         weigh(1, q_mx, 0)
-        for g in range(PASSES):
-            round_qm(0, g, by_scalar, qm_piece(0, g))
+        round_qm(0, 1, by_scalar, qm_piece(0, 1))
         weigh(1, q_mx, 1)
 
         def key_gradient(m, part):

@@ -30,7 +30,6 @@ SPREAD = P // 16
 KB = 1024
 PLACES = {
     "q1_grouped": 0, "ds0_128": 0, "ds0_256": 1 * KB,
-    "dk0_256": 4 * KB, "qm3_1_codes": 4 * KB,
     "gated1": 8 * KB,
     "qm_grouped2_0": 8 * KB, "qm_grouped2_1": 9 * KB, "qm_grouped3_0": 10 * KB, "qm_grouped3_1": 11 * KB,
     "dk1_256": 10 * KB,
@@ -288,14 +287,14 @@ def tile_attend_gat_lse_k_kernel(
             nc.vector.tensor_copy(windows[m][:].indirect(entries(part)), dk[:])
 
         def scatter_by_scalar(m, part, dk):
-            nc.scalar.activation(windows[m][:].indirect(entries(part)), dk[:], ACT.Copy)
+            nc.scalar.activation(windows[m][:].indirect(entries(part)), dk, ACT.Copy)
 
         def store(m):
             nc.sync.dma_start(out[m * P : (m + 1) * P, :], windows[m][:])
 
         def place_by_scalar(m):
             for half in HALVES:
-                scatter_by_scalar(m, half, dk_out(m, half, by_scalar))
+                scatter_by_scalar(m, half, dk_out(m, half, by_scalar)[:])
             store(m)
 
         second_quarter = ds_product(0, QUARTERS[1])
@@ -309,7 +308,7 @@ def tile_attend_gat_lse_k_kernel(
         second_block = sbuf("qm_grouped1", [P, PASSES, P, PACK], BF16, tag="neg_lse")
         for g in range(PASSES):
             round_qm(1, g, by_scalar, second_block[:, g])
-        scatter_by_scalar(0, HALVES[0], dk_out(0, HALVES[0], by_scalar))
+        scatter_by_scalar(0, HALVES[0], dk_out(0, HALVES[0], by_scalar)[:])
         third_quarter = ds_product(1, QUARTERS[2])
         last_quarter = ds_product(1, QUARTERS[3])
         ds_quantize(1, QUARTERS[2], third_quarter)
@@ -323,12 +322,18 @@ def tile_attend_gat_lse_k_kernel(
         for g in range(PASSES):
             quantize_qm(2, g)
         last_dk = dk_out(0, HALVES[1], by_vector)
-        quantize_qm(3, 0)
+        for g in range(PASSES):
+            quantize_qm(3, g)
         scatter_by_vector(0, HALVES[1], last_dk)
         store(0)
         place_by_scalar(1)
         dk = dk_out(2, slice(0, N), by_vector)
-        quantize_qm(3, 1)
         scatter_by_vector(2, slice(0, N), dk)
         store(2)
-        place_by_scalar(3)
+        acc = key_gradient(3, slice(0, N))
+        dk = sbuf("dk3", [P, N], F32)
+        for half in HALVES:
+            by_scalar(dk[:, half], acc[:, half])
+        for half in HALVES:
+            scatter_by_scalar(3, half, dk[:, half])
+        store(3)

@@ -218,8 +218,8 @@ def tile_attend_gat_lse_k_kernel(
         def round_qm(m, g, copy, grouped):
             qm_grouped[m, g] = grouped
             copy(
-                grouped.rearrange("p (c i) t -> p c t i", i=4),
-                qm_raw[m, g].rearrange("p t (c i) -> p c t i", i=4),
+                grouped.rearrange("p (c i) t -> p c t i", i=2),
+                qm_raw[m, g].rearrange("p t (c i) -> p c t i", i=2),
             )
 
         def qm_piece(m, g):

@@ -30,8 +30,9 @@ SPREAD = P // 16
 KB = 1024
 PLACES = {
     "q1_grouped": 0, "ds0_128": 0, "ds0_256": 1 * KB,
+    "dk0_256": 4 * KB, "qm3_1_codes": 4 * KB,
     "gated1": 8 * KB,
-    "qm_grouped2_0": 8 * KB, "qm_grouped2_1": 9 * KB, "qm_grouped3_0": 10 * KB, "qm_grouped3_1": 11 * KB,
+    "qm_grouped2_0": 8 * KB, "qm_grouped2_1": 9 * KB, "qm_grouped3_0": 10 * KB, "qm_grouped3_1": 9 * KB,
     "dk1_256": 10 * KB,
     "window3": 16 * KB + KB // 2, "v_pool_scales": 24 * KB,
     "q_raw0": 25 * KB, "k_pool_scales": 41 * KB, "k_pool_words": 41 * KB,
@@ -287,14 +288,14 @@ def tile_attend_gat_lse_k_kernel(
             nc.vector.tensor_copy(windows[m][:].indirect(entries(part)), dk[:])
 
         def scatter_by_scalar(m, part, dk):
-            nc.scalar.activation(windows[m][:].indirect(entries(part)), dk, ACT.Copy)
+            nc.scalar.activation(windows[m][:].indirect(entries(part)), dk[:], ACT.Copy)
 
         def store(m):
             nc.sync.dma_start(out[m * P : (m + 1) * P, :], windows[m][:])
 
         def place_by_scalar(m):
             for half in HALVES:
-                scatter_by_scalar(m, half, dk_out(m, half, by_scalar)[:])
+                scatter_by_scalar(m, half, dk_out(m, half, by_scalar))
             store(m)
 
         second_quarter = ds_product(0, QUARTERS[1])
@@ -308,7 +309,7 @@ def tile_attend_gat_lse_k_kernel(
         second_block = sbuf("qm_grouped1", [P, PASSES, P, PACK], BF16, tag="neg_lse")
         for g in range(PASSES):
             round_qm(1, g, by_scalar, second_block[:, g])
-        scatter_by_scalar(0, HALVES[0], dk_out(0, HALVES[0], by_scalar)[:])
+        scatter_by_scalar(0, HALVES[0], dk_out(0, HALVES[0], by_scalar))
         third_quarter = ds_product(1, QUARTERS[2])
         last_quarter = ds_product(1, QUARTERS[3])
         ds_quantize(1, QUARTERS[2], third_quarter)
@@ -316,24 +317,18 @@ def tile_attend_gat_lse_k_kernel(
         ds_quantize(1, QUARTERS[3], last_quarter)
         quantize_qm(1, 1)
 
-        for m in range(D_TILES // 2, D_TILES):
-            for g in range(PASSES):
-                round_qm(m, g, by_vector, qm_piece(m, g))
+        for m, g in ((2, 0), (2, 1), (3, 0)):
+            round_qm(m, g, by_vector, qm_piece(m, g))
         for g in range(PASSES):
             quantize_qm(2, g)
         last_dk = dk_out(0, HALVES[1], by_vector)
-        for g in range(PASSES):
-            quantize_qm(3, g)
+        quantize_qm(3, 0)
         scatter_by_vector(0, HALVES[1], last_dk)
         store(0)
         place_by_scalar(1)
+        round_qm(3, 1, by_vector, qm_piece(3, 1))
         dk = dk_out(2, slice(0, N), by_vector)
+        quantize_qm(3, 1)
         scatter_by_vector(2, slice(0, N), dk)
         store(2)
-        acc = key_gradient(3, slice(0, N))
-        dk = sbuf("dk3", [P, N], F32)
-        for half in HALVES:
-            by_scalar(dk[:, half], acc[:, half])
-        for half in HALVES:
-            scatter_by_scalar(3, half, dk[:, half])
-        store(3)
+        place_by_scalar(3)

from contextlib import ExitStack

import concourse.mybir as mybir

N, T, D, R = 512, 2048, 512, 1024
FLOPS = 3 * 2 * R * N * D

F32 = mybir.dt.float32
BF16 = mybir.dt.bfloat16
I32 = mybir.dt.int32
U32 = mybir.dt.uint32
U16 = mybir.dt.uint16
U8 = mybir.dt.uint8
E4M3 = mybir.dt.float8_e4m3fn_x4
E5M2 = mybir.dt.float8_e5m2_x4
ALU = mybir.AluOpType
ACT = mybir.ActivationFunctionType

P = 128
PACK = 4
K_PASS = P * PACK
PASSES = R // K_PASS
D_TILES = D // P
HALF = N // 2
HALVES = (slice(0, HALF), slice(HALF, N))
QUARTERS = tuple(slice(c * N // 4, (c + 1) * N // 4) for c in range(4))
RUN_PAIRS = (slice(0, 2), slice(2, PACK))
K_PLANE = 4
SPREAD = P // 16
KB = 1024
PLACES = {
    "q1_grouped": 0, "ds0_128": 0, "ds0_256": 1 * KB,
    "dk0_256": 4 * KB, "qm3_1_codes": 4 * KB,
    "gated1": 8 * KB,
    "qm_grouped2_0": 8 * KB, "qm_grouped2_1": 9 * KB, "qm_grouped3_0": 10 * KB, "qm_grouped3_1": 9 * KB,
    "dk1_256": 10 * KB,
    "window3": 16 * KB + KB // 2, "v_pool_scales": 24 * KB,
    "q_raw0": 25 * KB, "k_pool_scales": 41 * KB, "k_pool_words": 41 * KB,
    "v_pool_words": 52 * KB, "lse_q": 52 * KB,
    "do_raw1": 60 * KB, "q_raw1_0": 60 * KB, "q_raw1_256": 64 * KB,
    "qm_raw_first1": 25 * KB, "qm_raw0_0": 31 * KB, "weights1_0": 31 * KB,
    "qm_raw_later0": 41 * KB, "qm_raw_later1": 47 * KB,
    "ds0_0": 60 * KB,
}


def tile_attend_gat_lse_k_kernel(
    tc, qT, k_words, k_scales, v_words, v_scales, doT, lse, delta, rw, qm, offs, out
):
    nc = tc.nc
    with ExitStack() as ctx:
        keep = ctx.enter_context(tc.tile_pool(name="keep", bufs=1))
        placed = ctx.enter_context(tc.tile_pool(name="placed", bufs=1))
        psum = ctx.enter_context(tc.psum_pool(name="psum", bufs=1))

        def sbuf(name, shape, dtype, tag=None):
            if name in PLACES:
                return placed.tile(shape, dtype, name=name, align_bytes=64, offset=PLACES[name])
            return keep.tile(shape, dtype, name=name, tag=tag or name, align_bytes=64)

        def bank(index):
            return psum.tile([P, N], F32, name="bank%d" % index, tag="bank%d" % index)

        v_pool_scales = sbuf("v_pool_scales", [P, T // 4], I32)
        nc.gpsimd.memset(v_pool_scales[:], 0)
        k_pool_scales = sbuf("k_pool_scales", [P, T // 4], I32)
        nc.vector.memset(k_pool_scales[:], 0)
        v_plane = sbuf("v_plane", [P, N], U8)
        k_plane = sbuf("k_plane", [P, N], U8)
        for plane in (v_plane, k_plane):
            nc.gpsimd.memset(plane[:].bitcast(I32), 0)

        def zeroed_window(m):
            window = sbuf("window%d" % m, [P, T], F32)
            nc.vector.memset(window[:], 0.0)
            return window

        windows = [zeroed_window(m) for m in range(D_TILES - 1)]

        def by_partition(rows):
            return rows.rearrange("(p j) c -> p j c", j=PACK)

        def load_rows(name, rows):
            raw = sbuf(name, [P, PACK, rows.shape[1]], F32)
            nc.sync.dma_start(raw[:], by_partition(rows))
            return raw

        def load_per_query(name, values):
            columns = sbuf(name, [P, PASSES, 2 * PACK], F32)[:, :, 0:PACK]
            nc.sync.dma_start(columns, values[0].rearrange("(g p t) o -> p g (t o)", g=PASSES, t=PACK))
            return columns

        def load_pool_words(name, words):
            pool_words = sbuf(name, [P, T], I32)
            nc.sync.dma_start(pool_words[:], words[0].rearrange("p t j -> p (t j)").bitcast(I32))
            return pool_words

        def load_pool_scales(pool_scales, scales, first):
            nc.sync.dma_start(pool_scales[first:P:SPREAD, :], scales[0].bitcast(I32))

        def move_to_plane(plane, listed, first):
            for row in range(4):
                nc.sync.dma_start(
                    plane[first + row : P : 32, :].bitcast(I32),
                    listed[first + SPREAD * row : P : 32, :].bitcast(I32),
                )

        def entries(part):
            return offsets[:, part.start // 16 : part.stop // 16]

        def gather(name, window, dtype, part=slice(0, N)):
            listed = sbuf(name, [P, part.stop - part.start], dtype)
            nc.vector.tensor_copy(listed[:], window[:].bitcast(dtype).indirect(entries(part)))
            return listed

        def queries(g):
            return slice(g * K_PASS, (g + 1) * K_PASS)

        do_raw, q_raw = [None] * PASSES, [None] * PASSES
        offsets = keep.tile([P, N // 16], U16, name="offsets")
        nc.sync.dma_start(offsets[:], offs)
        delta_q = load_per_query("delta_q", delta)
        rw_q = load_per_query("rw_q", rw)
        do_raw[0] = sbuf("do_raw0", [P, PACK, K_PASS], F32)
        do_rows = by_partition(doT[0, :, queries(0)])
        for j in range(PACK - 1):
            nc.sync.dma_start(do_raw[0][:, j, :], do_rows[:, j, :])
        load_pool_scales(v_pool_scales, v_scales, 0)
        load_pool_scales(k_pool_scales, k_scales, K_PLANE)
        nc.sync.dma_start(do_raw[0][:, PACK - 1, :], do_rows[:, PACK - 1, :])
        v_pool_words = load_pool_words("v_pool_words", v_words)
        do_raw[1] = load_rows("do_raw1", doT[0, :, queries(1)])
        move_to_plane(v_plane, gather("v_scales", v_pool_scales, U8), 0)
        k_listed_scales = gather("k_scales", k_pool_scales, U8)
        windows.append(zeroed_window(D_TILES - 1))
        q_raw[0] = load_rows("q_raw0", qT[0, :, queries(0)])
        move_to_plane(k_plane, k_listed_scales, K_PLANE)
        k_pool_words = load_pool_words("k_pool_words", k_words)

        def mx_tiles(name, width):
            return sbuf(name + "_codes", [P, width], U32), sbuf(name + "_scales", [P, width], U8)

        def quantize(mx, columns, grouped, fmt):
            nc.vector.quantize_mx(out=mx[0][:, columns].bitcast(fmt), scales=mx[1][:, columns], in_=grouped)

        def grouped_tile(name):
            return sbuf(name + "_grouped", [P, PACK, P, PACK], BF16)

        def round_by_query(grouped, copy, raw, m_range=slice(0, P)):
            for runs in RUN_PAIRS:
                copy(
                    grouped[:].rearrange("p t m j -> p m j t")[:, m_range, :, runs],
                    raw[:].rearrange("p j (m t) -> p m j t", t=PACK)[:, :, :, runs],
                )

        def quantize_by_query(name, grouped, fmt):
            mx = mx_tiles(name, K_PASS)
            for runs in RUN_PAIRS:
                columns = slice(runs.start * P, runs.stop * P)
                quantize(mx, columns, grouped[:, runs].rearrange("p t m j -> p (t m j)"), fmt)
            return mx

        def multiply(acc, stationary, run, stationary_fmt, moving, moving_fmt, start, stop):
            columns = slice(run * P, (run + 1) * P)
            nc.tensor.matmul_mx(
                out=acc,
                lhsT=stationary[0][:, columns].bitcast(stationary_fmt),
                lhsT_scale=stationary[1][:, columns],
                rhs=moving[0][:].bitcast(moving_fmt),
                rhs_scale=moving[1][:],
                start=start,
                stop=stop,
            )

        gated = [sbuf("gated%d" % g, [P, PACK, N], F32) for g in range(PASSES)]
        weights = {}
        ds_mx = [mx_tiles("ds%d" % g, N) for g in range(PASSES)]

        def gate(g, do_mx):
            for t in range(PACK):
                dp = bank(PACK + t)
                multiply(dp[:], do_mx, t, E5M2, values, E4M3, True, True)
                nc.scalar.activation(
                    gated[g][:, t, :], dp[:], ACT.Identity,
                    bias=neg_delta_rw[:, g, t : t + 1], scale=rw_q[:, g, t : t + 1],
                )

        def weigh(g, q_mx, index, rounds=1):
            weights[g, index] = sbuf("weights%d_%d" % (g, index), [P, PACK, HALF], F32)
            moving = (k_listed_codes[index], k_plane[K_PLANE:, HALVES[index]])
            scores = [bank(PACK * index + t) for t in range(PACK)]
            width = HALF // rounds
            for first in range(0, HALF, width):
                for t in range(PACK):
                    if first == 0:
                        multiply(scores[t][:, 0:HALF], q_mx, t, E4M3, moving, E4M3, True, True)
                    nc.scalar.activation(
                        weights[g, index][:, t, first : first + width], scores[t][:, first : first + width],
                        ACT.Exp, bias=neg_lse[:, g, t : t + 1],
                    )

        def ds_product(g, part):
            width = part.stop - part.start
            index, first = divmod(part.start, HALF)
            ds = sbuf("ds%d_%d" % (g, part.start), [P, width, PACK], BF16)
            nc.vector.tensor_tensor(
                ds[:].rearrange("p (c i) t -> p c t i", i=2),
                weights[g, index][:, :, first : first + width].rearrange("p t (c i) -> p c t i", i=2),
                gated[g][:, :, part].rearrange("p t (c i) -> p c t i", i=2),
                ALU.mult,
            )
            return ds

        def ds_quantize(g, part, ds):
            quantize(ds_mx[g], part, ds[:].rearrange("p i t -> p (i t)"), E5M2)

        qm_grouped, qm_mx = {}, {}

        def round_qm(m, g, copy, grouped):
            qm_grouped[m, g] = grouped
            copy(
                grouped.rearrange("p (c i) t -> p c t i", i=2),
                qm_raw[m, g].rearrange("p t (c i) -> p c t i", i=2),
            )

        def qm_piece(m, g):
            return sbuf("qm_grouped%d_%d" % (m, g), [P, P, PACK], BF16)[:]

        def quantize_qm(m, g):
            qm_mx[m, g] = mx_tiles("qm%d_%d" % (m, g), P)
            quantize(qm_mx[m, g], slice(0, P), qm_grouped[m, g].rearrange("p d t -> p (d t)"), E4M3)

        by_scalar, by_vector = nc.scalar.copy, nc.vector.tensor_copy

        do_grouped = grouped_tile("do0")
        round_by_query(do_grouped, by_scalar, do_raw[0])
        do_mx = quantize_by_query("do0", do_grouped, E5M2)
        values = (gather("v_codes", v_pool_words, U32), v_plane)
        lse_q = load_per_query("lse_q", lse)
        neg_delta_rw = sbuf("neg_delta_rw", [P, PASSES, PACK], F32)
        nc.vector.scalar_tensor_tensor(neg_delta_rw[:], delta_q, -1.0, rw_q, ALU.mult, ALU.mult)
        gate(0, do_mx)
        do_grouped = grouped_tile("do1")
        round_by_query(do_grouped, by_vector, do_raw[1])
        gate(1, quantize_by_query("do1", do_grouped, E5M2))
        q_raw[1] = [load_rows("q_raw1_%d" % half.start, qT[0, :, queries(1)][:, half]) for half in HALVES]

        q_grouped = grouped_tile("q0")
        round_by_query(q_grouped, by_vector, q_raw[0])
        q_mx = quantize_by_query("q0", q_grouped, E4M3)
        qm_raw = {(0, 0): load_rows("qm_raw0_0", qm[0, queries(0), 0:P])[:]}
        first = load_rows("qm_raw_first1", qm[0, queries(1), 0 : D // 2])
        qm_raw.update({(m, 1): first[:, :, m * P : (m + 1) * P] for m in range(2)})
        k_listed_codes = [gather("k_codes%d" % half.start, k_pool_words, U32, half) for half in HALVES]
        for g in range(PASSES):
            done = 1 + g
            later = load_rows("qm_raw_later%d" % g, qm[0, queries(g), done * P : D])
            qm_raw.update({(m, g): later[:, :, (m - done) * P : (m - done + 1) * P] for m in range(done, D_TILES)})
        neg_lse = sbuf("neg_lse", [P, PASSES, PACK], F32)
        nc.scalar.mul(neg_lse[:], lse_q, -1.0)
        weigh(0, q_mx, 0, rounds=2)
        weigh(0, q_mx, 1)

        q_grouped = grouped_tile("q1")
        round_by_query(q_grouped, by_vector, q_raw[1][0], slice(0, P // 2))
        first_quarter = ds_product(0, QUARTERS[0])
        round_by_query(q_grouped, by_vector, q_raw[1][1], slice(P // 2, P))
        q_mx = quantize_by_query("q1", q_grouped, E4M3)
        ds_quantize(0, QUARTERS[0], first_quarter)
        round_qm(0, 0, by_scalar, qm_piece(0, 0))
        weigh(1, q_mx, 0)
        round_qm(0, 1, by_scalar, qm_piece(0, 1))
        weigh(1, q_mx, 1)

        def key_gradient(m, part):
            acc = bank(2 * m + part.start // HALF)[:, 0 : part.stop - part.start]
            for g in range(PASSES):
                moving = [tile[:, part] for tile in ds_mx[g]]
                multiply(acc, qm_mx[m, g], 0, E4M3, moving, E5M2, g == 0, g == PASSES - 1)
            return acc

        def dk_out(m, part, copy):
            dk = sbuf("dk%d_%d" % (m, part.start), [P, part.stop - part.start], F32)
            copy(dk[:], key_gradient(m, part))
            return dk

        def scatter_by_vector(m, part, dk):
            nc.vector.tensor_copy(windows[m][:].indirect(entries(part)), dk[:])

        def scatter_by_scalar(m, part, dk):
            nc.scalar.activation(windows[m][:].indirect(entries(part)), dk[:], ACT.Copy)

        def store(m):
            nc.sync.dma_start(out[m * P : (m + 1) * P, :], windows[m][:])

        def place_by_scalar(m):
            for half in HALVES:
                scatter_by_scalar(m, half, dk_out(m, half, by_scalar))
            store(m)

        second_quarter = ds_product(0, QUARTERS[1])
        second_half = ds_product(0, HALVES[1])
        ds_quantize(0, QUARTERS[1], second_quarter)
        first_half = ds_product(1, HALVES[0])
        for g in range(PASSES):
            quantize_qm(0, g)
        ds_quantize(1, HALVES[0], first_half)
        ds_quantize(0, HALVES[1], second_half)
        second_block = sbuf("qm_grouped1", [P, PASSES, P, PACK], BF16, tag="neg_lse")
        for g in range(PASSES):
            round_qm(1, g, by_scalar, second_block[:, g])
        scatter_by_scalar(0, HALVES[0], dk_out(0, HALVES[0], by_scalar))
        third_quarter = ds_product(1, QUARTERS[2])
        last_quarter = ds_product(1, QUARTERS[3])
        ds_quantize(1, QUARTERS[2], third_quarter)
        quantize_qm(1, 0)
        ds_quantize(1, QUARTERS[3], last_quarter)
        quantize_qm(1, 1)

        for m, g in ((2, 0), (2, 1), (3, 0)):
            round_qm(m, g, by_vector, qm_piece(m, g))
        for g in range(PASSES):
            quantize_qm(2, g)
        last_dk = dk_out(0, HALVES[1], by_vector)
        quantize_qm(3, 0)
        scatter_by_vector(0, HALVES[1], last_dk)
        store(0)
        place_by_scalar(1)
        round_qm(3, 1, by_vector, qm_piece(3, 1))
        dk = dk_out(2, slice(0, N), by_vector)
        quantize_qm(3, 1)
        scatter_by_vector(2, slice(0, N), dk)
        store(2)
        place_by_scalar(3)
